import numpy as np
import ml_dtypes


def mxq(x, axis, fmt="e4m3"):
    dtype, down = {"e4m3": (ml_dtypes.float8_e4m3fn, 7), "e5m2": (ml_dtypes.float8_e5m2, 14)}[fmt]
    v = np.moveaxis(np.asarray(x, np.float32).astype(ml_dtypes.bfloat16).astype(np.float64), axis, -1)
    blocks = v.reshape(v.shape[:-1] + (-1, 32))
    amax = np.abs(blocks).max(-1, keepdims=True)
    byte = np.maximum(np.where(amax > 0, np.frexp(amax)[1] - 1 + 127, 0) - down, 1)
    scale = np.exp2(byte - 127.0)
    codes = (blocks / scale).astype(np.float32).astype(dtype).astype(np.float64)
    return np.moveaxis((codes * scale).reshape(v.shape), -1, axis)


WIDE = False


def mx_kscale(k):
    if not WIDE:
        return np.ones(k)
    levels = np.array([18, -18])
    if k % 512:
        return np.exp2(np.random.permutation(np.resize(levels, k // 32))).repeat(32)
    a = np.empty((k // 512, 16))
    for p in range(k // 512):
        a[p, :8] = np.random.permutation(np.resize(levels, 8))
        for g in range(8):
            far = levels[np.abs(levels - a[p, g]) >= 10]
            a[p, g + 8] = far[np.random.randint(len(far))]
    return np.exp2(a.ravel()).repeat(32)


def f64(x):
    return np.asarray(x).astype(np.float64)


def striped(idx):
    return np.tile(np.asarray(idx).reshape(-1, 16).T, (8, 1)).astype(np.uint16)


def unstriped(offs):
    return offs[:16].T.reshape(-1).astype(np.int64)


def sig(x):
    return 1.0 / (1.0 + np.exp(-x))


def setup_inputs():
    n = np.random.standard_normal
    uni = np.random.uniform
    idx = np.random.permutation(2048)[:512]
    f_f = mx_kscale(512)
    f_i = np.ones(2048)
    f_i[idx] = mx_kscale(512)
    f_r = mx_kscale(512)
    return {
        "eT": (n((512, 2048)) * f_i[None, :]).astype(np.float32),
        "W": (n((512, 512)) / np.sqrt(512) * f_f[None, :]).astype(np.float32),
        "xT": (n((512, 512)) * f_r[None, :]).astype(np.float32),
        "G": (n((512, 512)) / np.sqrt(512) / f_r[:, None]).astype(np.float32),
        "hT": (1.5 * n((512, 2048))).astype(np.float32),
        "cf": (uni(0.75, 1.3, (512, 1)) / f_f[:, None]).astype(np.float32),
        "ts": np.tile(uni(0.75, 1.3, 2048) / f_i, (128, 1)).astype(np.float32),
        "offs": striped(idx),
    }


def reference(eT, W, xT, G, hT, cf, ts, offs):
    idx = unstriped(offs)
    eT_i = f64(eT)[:, idx]
    h = f64(hT)[:, idx]
    ts_i = f64(ts)[:1][:, idx]
    dv = mxq(f64(xT), 1, "e4m3") @ mxq(f64(G), 0, "e5m2")
    dz = f64(cf) * ts_i * dv * sig(h) * (1.0 + h * (1.0 - sig(h)))
    de = mxq(f64(W), 1, "e4m3") @ mxq(dz, 0, "e5m2")
    out_0 = np.zeros((512, 2048))
    out_0[:, idx] = de
    out_1 = mxq(eT_i, 1, "e4m3") @ mxq(dz, 1, "e5m2").T
    return out_0, out_1

@@ -1,0 +1,276 @@
+from contextlib import ExitStack
+
+import concourse.mybir as mybir
+from concourse.masks import make_identity
+
+F32 = mybir.dt.float32
+BF16 = mybir.dt.bfloat16
+U32 = mybir.dt.uint32
+U16 = mybir.dt.uint16
+U8 = mybir.dt.uint8
+E4M3 = mybir.dt.float8_e4m3fn_x4
+E5M2 = mybir.dt.float8_e5m2_x4
+ALU = mybir.AluOpType
+ACT = mybir.ActivationFunctionType
+
+P = 128
+PACK = 4
+N = 512
+HALF = N // 2
+ITEMS = 2048
+TILES = N // P
+WINDOWS = 3
+E_ON_SCALAR = (0, 2)
+
+KIB = 1024
+H_AT = [0, 8 * KIB, 16 * KIB, 24 * KIB]
+E_AT = [32 * KIB, 40 * KIB, 52 * KIB, 60 * KIB]
+E_HALF0_AT = 48 * KIB
+
+FLOPS = 3 * 2 * N * N * N
+BYTES = 4 * (3 * N * ITEMS + 4 * N * N + ITEMS + N) + 2 * P * (N // 16)
+
+
+def tile_attend_gtower_sil_EW_kernel(tc, eT, W, xT, G, hT, cf, ts, offs, out_0, out_1):
+    nc = tc.nc
+    with ExitStack() as ctx:
+        lists = ctx.enter_context(tc.tile_pool(name="lists", bufs=1))
+        sb = ctx.enter_context(tc.tile_pool(name="sb", bufs=1))
+        arena = ctx.enter_context(tc.tile_pool(name="arena", bufs=1))
+        ps = ctx.enter_context(tc.psum_pool(name="ps", bufs=1))
+
+        def sbuf(shape, dtype, name, tag=None):
+            if isinstance(tag, int):
+                return arena.tile(shape, dtype, name=name, align_bytes=64, offset=tag)
+            return sb.tile(shape, dtype, name=name, tag=tag or name, align_bytes=64)
+
+        def psum(shape, name, tag):
+            return ps.tile(shape, F32, name=name, tag=tag)
+
+        def mx_tiles(width, name, tag=None):
+            return sbuf([P, width], U32, name + "_codes", tag), sbuf([P, width], U8, name + "_scales")
+
+        def quantise(mx, cols, woven, fmt):
+            nc.vector.quantize_mx(
+                out=mx[0][:, cols].bitcast(fmt), scales=mx[1][:, cols], in_=woven[:].rearrange("p c j -> p (c j)")
+            )
+
+        def multiply(acc, still, still_cols, still_fmt, moving, moving_fmt):
+            nc.tensor.matmul_mx(
+                out=acc,
+                lhsT=still[0][:, still_cols].bitcast(still_fmt),
+                lhsT_scale=still[1][:, still_cols],
+                rhs=moving[0][:].bitcast(moving_fmt),
+                rhs_scale=moving[1][:],
+                start=True,
+                stop=True,
+            )
+
+        def turn_f32(src, turned, woven):
+            for j in range(PACK):
+                nc.tensor.transpose(turned[:, j, :], src[:, j:N:PACK], ident[:])
+            nc.scalar.copy(woven, turned.rearrange("s j m -> s m j"))
+
+        def block(c):
+            return slice(c * P, (c + 1) * P)
+
+        def half(a):
+            return slice(a * HALF, (a + 1) * HALF)
+
+        everything = slice(0, N)
+
+        offsets = lists.tile([P, N // 16], U16, name="offsets")
+        nc.sync.dma_start(offsets[:], offs)
+
+        h_rows = hT.rearrange("(p t) n -> t p n", t=PACK)
+        h_win = [sbuf([P, ITEMS], F32, "h_win%d" % t, H_AT[t]) for t in range(PACK)]
+        x_rows = xT.rearrange("(p a t) r -> a p t r", a=2, t=2)
+        x_raw = [sbuf([P, 2, N], F32, "x_raw%d" % a) for a in range(2)]
+        g_rows = G.rearrange("(p j) i -> p j i", j=PACK)
+        g_raw = [sbuf([P, PACK, HALF], F32, "g_raw%d" % a) for a in range(2)]
+        w_raw = [sbuf([P, N], F32, "w_raw%d" % c) for c in range(TILES)]
+        e_win = [sbuf([P, ITEMS], F32, "e_win%d" % c, E_AT[c]) for c in range(TILES)]
+        ts_win = sbuf([P, ITEMS], F32, "ts_win")
+        cf_col = sbuf([P, PACK], F32, "cf_col")
+
+        nc.vector.memset(ts_win[:], 0.0)
+        nc.sync.dma_start(h_win[0][:], h_rows[0])
+        nc.sync.dma_start(ts_win[0:1, :], ts[0:1, :])
+        nc.scalar.dma_start(cf_col[:], cf.rearrange("(p t) o -> p (t o)", t=PACK))
+        for a in range(2):
+            nc.sync.dma_start(x_raw[a][:], x_rows[a])
+        nc.sync.dma_start(g_raw[0][:], g_rows[:, :, half(0)])
+        nc.sync.dma_start(h_win[1][:], h_rows[1])
+        nc.sync.dma_start(g_raw[1][:], g_rows[:, :, half(1)])
+        nc.sync.dma_start(h_win[2][:], h_rows[2])
+        nc.sync.dma_start(h_win[3][:], h_rows[3])
+        for c in range(TILES):
+            nc.sync.dma_start(w_raw[c][:], W[block(c), :])
+        for c in range(TILES):
+            nc.sync.dma_start(e_win[c][:], eT[block(c), :])
+
+        ident = sbuf([P, P], F32, "ident")
+        make_identity(nc, ident[:])
+        windows = [sbuf([P, ITEMS], F32, "window%d" % w) for w in range(WINDOWS)]
+        for window in windows:
+            nc.gpsimd.memset(window[:], 0.0)
+
+        ts_row = sbuf([P, N], F32, "ts_row")
+        nc.vector.tensor_copy(ts_row[:], ts_win[:].indirect(offsets[:]))
+
+        slope = [sbuf([P, N], F32, "slope%d" % t) for t in range(PACK)]
+
+        def make_slope(t, h_tag=None, a_tag=None, s_tag=None):
+            h = sbuf([P, N], F32, "h%d" % t, h_tag)
+            nc.vector.tensor_copy(h[:], h_win[t][:].indirect(offsets[:]))
+            s = sbuf([P, N], F32, "s%d" % t, s_tag)
+            a = sbuf([P, N], F32, "a%d" % t, a_tag)
+            nc.scalar.activation(s[:], h[:], ACT.Sigmoid)
+            nc.vector.scalar_tensor_tensor(a[:], s[:], 1.0, h[:], ALU.subtract, ALU.mult)
+            nc.vector.scalar_tensor_tensor(slope[t][:], a[:], 1.0, s[:], ALU.subtract, ALU.mult)
+
+        make_slope(0)
+
+        x_woven = sbuf([P, N, PACK], BF16, "x_woven")
+        x_woven_words = x_woven[:].rearrange("s f r -> s (f r)").bitcast(F32).rearrange("s (t m u) -> s t m u", t=PACK, u=2)
+        for a in range(2):
+            x_half = sbuf([P, 2 * N], BF16, "x_half%d" % a)
+            nc.scalar.copy(x_half[:], x_raw[a][:].rearrange("p t r -> p (t r)"))
+            x_words = x_half[:].bitcast(F32).rearrange("p (t w) -> p t w", t=2)
+            turned = psum([P, 2, 2, P], "x_turned%d" % a, "one%d" % a)
+            for t in range(2):
+                for u in range(2):
+                    nc.tensor.transpose(turned[:, t, u, :], x_words[:, t, u:HALF:2], ident[:])
+            nc.scalar.copy(x_woven_words[:, 2 * a : 2 * a + 2, :, :], turned[:].rearrange("s t u m -> s t m u"))
+        ts_turned = psum([P, TILES, P], "ts_turned", "one1")
+        for c in range(TILES):
+            nc.tensor.transpose(ts_turned[:, c, :], ts_row[:, block(c)], ident[:])
+        ts_col = sbuf([P, TILES], F32, "ts_col")
+        nc.scalar.activation(ts_col[:], ts_turned[:, :, 0], ACT.Copy, scale=-1.0)
+        g_mx = mx_tiles(N, "g")
+        g_woven = [sbuf([P, HALF, PACK], BF16, "g_woven0", "h0"), sbuf([P, HALF, PACK], BF16, "g_woven1", H_AT[1])]
+        nc.vector.tensor_copy(g_woven[0][:], g_raw[0][:].rearrange("p j i -> p i j"))
+        quantise(g_mx, half(0), g_woven[0], E5M2)
+        x_mx = mx_tiles(N, "x", "h0")
+        quantise(x_mx, everything, x_woven, E4M3)
+        make_slope(1, "x_woven")
+        nc.vector.tensor_copy(g_woven[1][:], g_raw[1][:].rearrange("p j i -> p i j"))
+        quantise(g_mx, half(1), g_woven[1], E5M2)
+
+        dv_ts = [sbuf([P, N], F32, "dv_ts%d" % c) for c in range(TILES)]
+        dv_t = psum([P, TILES, N], "dv_t", "four")
+        for c in range(TILES):
+            multiply(dv_t[:, c, :], g_mx, block(c), E5M2, x_mx, E4M3)
+            nc.scalar.activation(dv_ts[c][:], dv_t[:, c, :], ACT.Copy, scale=ts_col[:, c : c + 1])
+        make_slope(2, H_AT[1], H_AT[3], "ts_col")
+        dv = [psum([P, N], "dv%d" % t, "one%d" % t) for t in range(PACK)]
+        for c in range(TILES):
+            for t in range(PACK):
+                nc.tensor.transpose(dv[t][:, block(c)], dv_ts[c][:, block(t)], ident[:])
+        make_slope(3, H_AT[2])
+
+        dz = sbuf([P, PACK, N], BF16, "dz", H_AT[3] + 2 * KIB)
+        for t in range(PACK):
+            nc.vector.scalar_tensor_tensor(dz[:, t, :], dv[t][:], cf_col[:, t : t + 1], slope[t][:], ALU.mult, ALU.mult)
+
+        dz_f = [sbuf([P, HALF, PACK], BF16, "dz_f%d" % a) for a in range(2)]
+        dz_it = dz[:].rearrange("p t i -> p i t")
+        for a in range(2):
+            nc.vector.tensor_copy(dz_f[a][:], dz_it[:, half(a), :])
+
+        w_woven = [sbuf([P, HALF, PACK], BF16, "w_woven0"), sbuf([P, HALF, PACK], BF16, "w_woven1", E_AT[0])]
+        w_turned = psum([P, TILES, PACK, P], "w_turned", "four")
+        e_half = {}
+
+        def cast_e(c, tag=None):
+            e_half[c] = sbuf([P, ITEMS], BF16, "e_half%d" % c, tag)
+            nc.scalar.activation(e_half[c][:], e_win[c][:], ACT.Copy)
+
+        for c in range(TILES):
+            if c == 2:
+                cast_e(0, E_HALF0_AT)
+            turn_f32(w_raw[c], w_turned[:, c, :, :], w_woven[c // 2][:, block(c % 2), :])
+        w_mx = [mx_tiles(HALF, "w0", "slope3")]
+        quantise(w_mx[0], half(0), w_woven[0], E4M3)
+
+        dzf_mx = mx_tiles(N, "dzf")
+        for a in range(2):
+            quantise(dzf_mx, half(a), dz_f[a], E5M2)
+
+        e = {}
+
+        def gather_e(c, tag=None):
+            e[c] = sbuf([P, N], BF16, "e%d" % c, tag)
+            if c in E_ON_SCALAR:
+                nc.scalar.activation(e[c][:], e_half[c][:].indirect(offsets[:]), ACT.Copy)
+            else:
+                nc.vector.tensor_copy(e[c][:], e_win[c][:].indirect(offsets[:]))
+
+        def turn_e(c, bank):
+            e_words = e[c][:].bitcast(F32)
+            turned = psum([P, 2, P], "e_turned%d" % c, bank)
+            for u in range(2):
+                nc.tensor.transpose(turned[:, u, :], e_words[:, u:HALF:2], ident[:])
+            e_woven = sbuf([P, P, PACK], BF16, "e_woven%d" % c)
+            e_woven_words = e_woven[:].rearrange("s d r -> s (d r)").bitcast(F32).rearrange("s (d u) -> s d u", u=2)
+            nc.scalar.copy(e_woven_words, turned[:].rearrange("s u m -> s m u"))
+            return e_woven
+
+        de = {}
+
+        def table_gradient(c, tag=None):
+            de_acc = psum([P, N], "de_acc%d" % c, "one%d" % c)
+            multiply(de_acc[:], w_mx[c // 2], block(c % 2), E4M3, dzf_mx, E5M2)
+            de[c] = sbuf([P, N], F32, "de%d" % c, tag)
+            nc.scalar.copy(de[c][:], de_acc[:])
+
+        gather_e(0, "w_raw3")
+        gather_e(1, "dz_f1")
+        table_gradient(0, E_HALF0_AT - KIB)
+        table_gradient(1)
+        w_mx.append(mx_tiles(HALF, "w1", E_AT[1]))
+        quantise(w_mx[1], half(0), w_woven[1], E4M3)
+        table_gradient(2)
+        table_gradient(3)
+
+        dz_i = sbuf([P, N, PACK], BF16, "dz_i")
+        dz_words = dz[:].bitcast(F32)
+        dz_i_words = dz_i[:].rearrange("s f r -> s (f r)").bitcast(F32).rearrange("s (p t u) -> s p t u", t=PACK, u=2)
+        for b in range(2):
+            turned = psum([P, 2, 2, P], "dz_turned%d" % b, "one%d" % b)
+            for t in range(2):
+                for u in range(2):
+                    nc.tensor.transpose(turned[:, t, u, :], dz_words[:, 2 * b + t, u:HALF:2], ident[:])
+            nc.scalar.copy(dz_i_words[:, :, 2 * b : 2 * b + 2, :], turned[:].rearrange("s t u p -> s p t u"))
+
+        def scatter(c):
+            window = windows[c % WINDOWS]
+            nc.vector.tensor_copy(window[:].indirect(offsets[:]), de[c][:])
+            nc.sync.dma_start(out_0[block(c), :], window[:])
+
+        def weight_gradient(c, e_woven, tag=None):
+            e_mx = mx_tiles(P, "e%d" % c, tag)
+            quantise(e_mx, block(0), e_woven, E4M3)
+            acc = psum([P, N], "dw_acc%d" % c, "one%d" % c)
+            multiply(acc[:], e_mx, block(0), E4M3, dzi_mx, E5M2)
+            dw = sbuf([P, N], F32, "dw%d" % c)
+            nc.scalar.copy(dw[:], acc[:])
+            nc.scalar.dma_start(out_1[block(c), :], dw[:])
+
+        e1_woven = turn_e(1, "four")
+        e0_woven = turn_e(0, "one2")
+        scatter(0)
+        scatter(1)
+        scatter(2)
+        cast_e(2)
+        gather_e(2)
+        e2_woven = turn_e(2, "four")
+        dzi_mx = mx_tiles(N, "dzi")
+        quantise(dzi_mx, everything, dz_i, E5M2)
+        weight_gradient(0, e0_woven)
+        weight_gradient(1, e1_woven)
+        gather_e(3)
+        weight_gradient(2, e2_woven)
+        e3_woven = turn_e(3, "four")
+        scatter(3)
+        weight_gradient(3, e3_woven, "de3")

@@ -19,7 +19,7 @@ N = 512
 HALF = N // 2
 ITEMS = 2048
 TILES = N // P
-WINDOWS = 3
+WINDOWS = 2
 E_ON_SCALAR = (0, 2)
 
 KIB = 1024
@@ -88,7 +88,9 @@ def tile_attend_gtower_sil_EW_kernel(tc, eT, W, xT, G, hT, cf, ts, offs, out_0, 
         x_raw = [sbuf([P, 2, N], F32, "x_raw%d" % a) for a in range(2)]
         g_rows = G.rearrange("(p j) i -> p j i", j=PACK)
         g_raw = [sbuf([P, PACK, HALF], F32, "g_raw%d" % a) for a in range(2)]
-        w_raw = [sbuf([P, N], F32, "w_raw%d" % c) for c in range(TILES)]
+        w_rows = W.rearrange("(p a c) f -> a p c f", a=2, c=2)
+        w_raw = [sbuf([P, 2, N], F32, "w_raw%d" % a) for a in range(2)]
+        out_0_rows = out_0.rearrange("(p c) n -> c p n", c=TILES)
         e_win = [sbuf([P, ITEMS], F32, "e_win%d" % c, E_AT[c]) for c in range(TILES)]
         ts_win = sbuf([P, ITEMS], F32, "ts_win")
         cf_col = sbuf([P, PACK], F32, "cf_col")
@@ -104,8 +106,8 @@ def tile_attend_gtower_sil_EW_kernel(tc, eT, W, xT, G, hT, cf, ts, offs, out_0, 
         nc.sync.dma_start(g_raw[1][:], g_rows[:, :, half(1)])
         nc.sync.dma_start(h_win[2][:], h_rows[2])
         nc.sync.dma_start(h_win[3][:], h_rows[3])
-        for c in range(TILES):
-            nc.sync.dma_start(w_raw[c][:], W[block(c), :])
+        for a in range(2):
+            nc.sync.dma_start(w_raw[a][:], w_rows[a])
         for c in range(TILES):
             nc.sync.dma_start(e_win[c][:], eT[block(c), :])
 
@@ -113,7 +115,7 @@ def tile_attend_gtower_sil_EW_kernel(tc, eT, W, xT, G, hT, cf, ts, offs, out_0, 
         make_identity(nc, ident[:])
         windows = [sbuf([P, ITEMS], F32, "window%d" % w) for w in range(WINDOWS)]
         for window in windows:
-            nc.gpsimd.memset(window[:], 0.0)
+            nc.vector.memset(window[:], 0.0)
 
         ts_row = sbuf([P, N], F32, "ts_row")
         nc.vector.tensor_copy(ts_row[:], ts_win[:].indirect(offsets[:]))
@@ -189,7 +191,7 @@ def tile_attend_gtower_sil_EW_kernel(tc, eT, W, xT, G, hT, cf, ts, offs, out_0, 
         for c in range(TILES):
             if c == 2:
                 cast_e(0, E_HALF0_AT)
-            turn_f32(w_raw[c], w_turned[:, c, :, :], w_woven[c // 2][:, block(c % 2), :])
+            turn_f32(w_raw[c // 2][:, c % 2, :], w_turned[:, c, :, :], w_woven[c // 2][:, block(c % 2), :])
         w_mx = [mx_tiles(HALF, "w0", "slope3")]
         quantise(w_mx[0], half(0), w_woven[0], E4M3)
 
@@ -218,20 +220,20 @@ def tile_attend_gtower_sil_EW_kernel(tc, eT, W, xT, G, hT, cf, ts, offs, out_0, 
 
         de = {}
 
-        def table_gradient(c, tag=None):
+        def table_gradient(c, target):
             de_acc = psum([P, N], "de_acc%d" % c, "one%d" % c)
             multiply(de_acc[:], w_mx[c // 2], block(c % 2), E4M3, dzf_mx, E5M2)
-            de[c] = sbuf([P, N], F32, "de%d" % c, tag)
-            nc.scalar.copy(de[c][:], de_acc[:])
+            de[c] = target
+            nc.scalar.copy(target, de_acc[:])
 
-        gather_e(0, "w_raw3")
+        gather_e(0, "w_raw1")
         gather_e(1, "dz_f1")
-        table_gradient(0, E_HALF0_AT - KIB)
-        table_gradient(1)
+        de01 = sbuf([P, 2, N], F32, "de01", E_HALF0_AT - 2 * KIB)
+        table_gradient(0, de01[:, 0, :])
+        table_gradient(1, de01[:, 1, :])
         w_mx.append(mx_tiles(HALF, "w1", E_AT[1]))
         quantise(w_mx[1], half(0), w_woven[1], E4M3)
-        table_gradient(2)
-        table_gradient(3)
+        table_gradient(2, sbuf([P, N], F32, "de2")[:])
 
         dz_i = sbuf([P, N, PACK], BF16, "dz_i")
         dz_words = dz[:].bitcast(F32)
@@ -245,13 +247,13 @@ def tile_attend_gtower_sil_EW_kernel(tc, eT, W, xT, G, hT, cf, ts, offs, out_0, 
 
         def scatter(c):
             window = windows[c % WINDOWS]
-            nc.vector.tensor_copy(window[:].indirect(offsets[:]), de[c][:])
-            nc.sync.dma_start(out_0[block(c), :], window[:])
+            nc.vector.tensor_copy(window[:].indirect(offsets[:]), de[c])
+            nc.sync.dma_start(out_0_rows[c], window[:])
 
-        def weight_gradient(c, e_woven, tag=None):
+        def weight_gradient(c, e_woven, bank, tag=None):
             e_mx = mx_tiles(P, "e%d" % c, tag)
             quantise(e_mx, block(0), e_woven, E4M3)
-            acc = psum([P, N], "dw_acc%d" % c, "one%d" % c)
+            acc = psum([P, N], "dw_acc%d" % c, bank)
             multiply(acc[:], e_mx, block(0), E4M3, dzi_mx, E5M2)
             dw = sbuf([P, N], F32, "dw%d" % c)
             nc.scalar.copy(dw[:], acc[:])
@@ -264,13 +266,14 @@ def tile_attend_gtower_sil_EW_kernel(tc, eT, W, xT, G, hT, cf, ts, offs, out_0, 
         scatter(2)
         cast_e(2)
         gather_e(2)
-        e2_woven = turn_e(2, "four")
-        dzi_mx = mx_tiles(N, "dzi")
-        quantise(dzi_mx, everything, dz_i, E5M2)
-        weight_gradient(0, e0_woven)
-        weight_gradient(1, e1_woven)
+        e2_woven = turn_e(2, "one0")
         gather_e(3)
-        weight_gradient(2, e2_woven)
+        table_gradient(3, sbuf([P, N], F32, "de3", E_AT[3])[:])
+        dzi_mx = mx_tiles(N, "dzi", E_AT[3] + 2 * KIB)
+        quantise(dzi_mx, everything, dz_i, E5M2)
         e3_woven = turn_e(3, "four")
+        weight_gradient(0, e0_woven, "one0")
+        weight_gradient(1, e1_woven, "one0")
+        weight_gradient(2, e2_woven, "one1")
         scatter(3)
-        weight_gradient(3, e3_woven, "de3")
+        weight_gradient(3, e3_woven, "one3", E_AT[3])

@@ -19,13 +19,14 @@ N = 512
 HALF = N // 2
 ITEMS = 2048
 TILES = N // P
-WINDOWS = 2
+WINDOWS = 3
 E_ON_SCALAR = (0, 2)
 
 KIB = 1024
 H_AT = [0, 8 * KIB, 16 * KIB, 24 * KIB]
-E_AT = [32 * KIB, 40 * KIB, 52 * KIB, 60 * KIB]
-E_HALF0_AT = 48 * KIB
+E_AT = [32 * KIB, 40 * KIB, 48 * KIB, 56 * KIB]
+E_END = 64 * KIB
+E_HALF_AT = 66 * KIB
 
 FLOPS = 3 * 2 * N * N * N
 BYTES = 4 * (3 * N * ITEMS + 4 * N * N + ITEMS + N) + 2 * P * (N // 16)
@@ -84,8 +85,8 @@ def tile_attend_gtower_sil_EW_kernel(tc, eT, W, xT, G, hT, cf, ts, offs, out_0, 
 
         h_rows = hT.rearrange("(p t) n -> t p n", t=PACK)
         h_win = [sbuf([P, ITEMS], F32, "h_win%d" % t, H_AT[t]) for t in range(PACK)]
-        x_rows = xT.rearrange("(p a t) r -> a p t r", a=2, t=2)
-        x_raw = [sbuf([P, 2, N], F32, "x_raw%d" % a) for a in range(2)]
+        x_rows = xT.rearrange("(p t) r -> t p r", t=PACK)
+        x_raw = [sbuf([P, N], F32, "x_raw%d" % t) for t in range(PACK)]
         g_rows = G.rearrange("(p j) i -> p j i", j=PACK)
         g_raw = [sbuf([P, PACK, HALF], F32, "g_raw%d" % a) for a in range(2)]
         w_rows = W.rearrange("(p a c) f -> a p c f", a=2, c=2)
@@ -99,8 +100,8 @@ def tile_attend_gtower_sil_EW_kernel(tc, eT, W, xT, G, hT, cf, ts, offs, out_0, 
         nc.sync.dma_start(h_win[0][:], h_rows[0])
         nc.sync.dma_start(ts_win[0:1, :], ts[0:1, :])
         nc.scalar.dma_start(cf_col[:], cf.rearrange("(p t) o -> p (t o)", t=PACK))
-        for a in range(2):
-            nc.sync.dma_start(x_raw[a][:], x_rows[a])
+        for t in range(PACK):
+            nc.sync.dma_start(x_raw[t][:], x_rows[t])
         nc.sync.dma_start(g_raw[0][:], g_rows[:, :, half(0)])
         nc.sync.dma_start(h_win[1][:], h_rows[1])
         nc.sync.dma_start(g_raw[1][:], g_rows[:, :, half(1)])
@@ -115,10 +116,7 @@ def tile_attend_gtower_sil_EW_kernel(tc, eT, W, xT, G, hT, cf, ts, offs, out_0, 
         make_identity(nc, ident[:])
         windows = [sbuf([P, ITEMS], F32, "window%d" % w) for w in range(WINDOWS)]
         for window in windows:
-            nc.vector.memset(window[:], 0.0)
-
-        ts_row = sbuf([P, N], F32, "ts_row")
-        nc.vector.tensor_copy(ts_row[:], ts_win[:].indirect(offsets[:]))
+            nc.gpsimd.memset(window[:], 0.0)
 
         slope = [sbuf([P, N], F32, "slope%d" % t) for t in range(PACK)]
 
@@ -133,18 +131,20 @@ def tile_attend_gtower_sil_EW_kernel(tc, eT, W, xT, G, hT, cf, ts, offs, out_0, 
 
         make_slope(0)
 
+        ts_row = sbuf([P, N], F32, "ts_row")
+        nc.vector.tensor_copy(ts_row[:], ts_win[:].indirect(offsets[:]))
+
         x_woven = sbuf([P, N, PACK], BF16, "x_woven")
         x_woven_words = x_woven[:].rearrange("s f r -> s (f r)").bitcast(F32).rearrange("s (t m u) -> s t m u", t=PACK, u=2)
-        for a in range(2):
-            x_half = sbuf([P, 2 * N], BF16, "x_half%d" % a)
-            nc.scalar.copy(x_half[:], x_raw[a][:].rearrange("p t r -> p (t r)"))
-            x_words = x_half[:].bitcast(F32).rearrange("p (t w) -> p t w", t=2)
-            turned = psum([P, 2, 2, P], "x_turned%d" % a, "one%d" % a)
-            for t in range(2):
-                for u in range(2):
-                    nc.tensor.transpose(turned[:, t, u, :], x_words[:, t, u:HALF:2], ident[:])
-            nc.scalar.copy(x_woven_words[:, 2 * a : 2 * a + 2, :, :], turned[:].rearrange("s t u m -> s t m u"))
-        ts_turned = psum([P, TILES, P], "ts_turned", "one1")
+        for t in range(PACK):
+            x_half = sbuf([P, N], BF16, "x_half%d" % t)
+            nc.scalar.copy(x_half[:], x_raw[t][:])
+            x_words = x_half[:].bitcast(F32)
+            turned = psum([P, 2, P], "x_turned%d" % t, "one%d" % t)
+            for u in range(2):
+                nc.tensor.transpose(turned[:, u, :], x_words[:, u:HALF:2], ident[:])
+            nc.scalar.copy(x_woven_words[:, t, :, :], turned[:].rearrange("s u m -> s m u"))
+        ts_turned = psum([P, TILES, P], "ts_turned", "one2")
         for c in range(TILES):
             nc.tensor.transpose(ts_turned[:, c, :], ts_row[:, block(c)], ident[:])
         ts_col = sbuf([P, TILES], F32, "ts_col")
@@ -164,14 +164,14 @@ def tile_attend_gtower_sil_EW_kernel(tc, eT, W, xT, G, hT, cf, ts, offs, out_0, 
         for c in range(TILES):
             multiply(dv_t[:, c, :], g_mx, block(c), E5M2, x_mx, E4M3)
             nc.scalar.activation(dv_ts[c][:], dv_t[:, c, :], ACT.Copy, scale=ts_col[:, c : c + 1])
-        make_slope(2, H_AT[1], H_AT[3], "ts_col")
+        make_slope(2, H_AT[1], H_AT[3])
         dv = [psum([P, N], "dv%d" % t, "one%d" % t) for t in range(PACK)]
         for c in range(TILES):
             for t in range(PACK):
                 nc.tensor.transpose(dv[t][:, block(c)], dv_ts[c][:, block(t)], ident[:])
         make_slope(3, H_AT[2])
 
-        dz = sbuf([P, PACK, N], BF16, "dz", H_AT[3] + 2 * KIB)
+        dz = sbuf([P, PACK, N], BF16, "dz", H_AT[2])
         for t in range(PACK):
             nc.vector.scalar_tensor_tensor(dz[:, t, :], dv[t][:], cf_col[:, t : t + 1], slope[t][:], ALU.mult, ALU.mult)
 
@@ -184,13 +184,13 @@ def tile_attend_gtower_sil_EW_kernel(tc, eT, W, xT, G, hT, cf, ts, offs, out_0, 
         w_turned = psum([P, TILES, PACK, P], "w_turned", "four")
         e_half = {}
 
-        def cast_e(c, tag=None):
-            e_half[c] = sbuf([P, ITEMS], BF16, "e_half%d" % c, tag)
+        def cast_e(c):
+            e_half[c] = sbuf([P, ITEMS], BF16, "e_half%d" % c, E_HALF_AT)
             nc.scalar.activation(e_half[c][:], e_win[c][:], ACT.Copy)
 
         for c in range(TILES):
             if c == 2:
-                cast_e(0, E_HALF0_AT)
+                cast_e(0)
             turn_f32(w_raw[c // 2][:, c % 2, :], w_turned[:, c, :, :], w_woven[c // 2][:, block(c % 2), :])
         w_mx = [mx_tiles(HALF, "w0", "slope3")]
         quantise(w_mx[0], half(0), w_woven[0], E4M3)
@@ -208,12 +208,12 @@ def tile_attend_gtower_sil_EW_kernel(tc, eT, W, xT, G, hT, cf, ts, offs, out_0, 
             else:
                 nc.vector.tensor_copy(e[c][:], e_win[c][:].indirect(offsets[:]))
 
-        def turn_e(c, bank):
+        def turn_e(c, bank, at=None):
             e_words = e[c][:].bitcast(F32)
             turned = psum([P, 2, P], "e_turned%d" % c, bank)
             for u in range(2):
                 nc.tensor.transpose(turned[:, u, :], e_words[:, u:HALF:2], ident[:])
-            e_woven = sbuf([P, P, PACK], BF16, "e_woven%d" % c)
+            e_woven = sbuf([P, P, PACK], BF16, "e_woven%d" % c, at)
             e_woven_words = e_woven[:].rearrange("s d r -> s (d r)").bitcast(F32).rearrange("s (d u) -> s d u", u=2)
             nc.scalar.copy(e_woven_words, turned[:].rearrange("s u m -> s m u"))
             return e_woven
@@ -226,14 +226,13 @@ def tile_attend_gtower_sil_EW_kernel(tc, eT, W, xT, G, hT, cf, ts, offs, out_0, 
             de[c] = target
             nc.scalar.copy(target, de_acc[:])
 
-        gather_e(0, "w_raw1")
         gather_e(1, "dz_f1")
-        de01 = sbuf([P, 2, N], F32, "de01", E_HALF0_AT - 2 * KIB)
+        de01 = sbuf([P, 2, N], F32, "de01", E_AT[1] - 2 * KIB)
         table_gradient(0, de01[:, 0, :])
         table_gradient(1, de01[:, 1, :])
-        w_mx.append(mx_tiles(HALF, "w1", E_AT[1]))
+        w_mx.append(mx_tiles(HALF, "w1", E_AT[1] + 2 * KIB))
         quantise(w_mx[1], half(0), w_woven[1], E4M3)
-        table_gradient(2, sbuf([P, N], F32, "de2")[:])
+        gather_e(0, "slope3")
 
         dz_i = sbuf([P, N, PACK], BF16, "dz_i")
         dz_words = dz[:].bitcast(F32)
@@ -250,30 +249,38 @@ def tile_attend_gtower_sil_EW_kernel(tc, eT, W, xT, G, hT, cf, ts, offs, out_0, 
             nc.vector.tensor_copy(window[:].indirect(offsets[:]), de[c])
             nc.sync.dma_start(out_0_rows[c], window[:])
 
-        def weight_gradient(c, e_woven, bank, tag=None):
-            e_mx = mx_tiles(P, "e%d" % c, tag)
-            quantise(e_mx, block(0), e_woven, E4M3)
+        e_mx = {}
+
+        def quantise_e(c):
+            e_mx[c] = mx_tiles(P, "e%d" % c)
+            quantise(e_mx[c], block(0), e_woven[c], E4M3)
+
+        def weight_gradient(c, bank, dw_at=None):
             acc = psum([P, N], "dw_acc%d" % c, bank)
-            multiply(acc[:], e_mx, block(0), E4M3, dzi_mx, E5M2)
-            dw = sbuf([P, N], F32, "dw%d" % c)
+            multiply(acc[:], e_mx[c], block(0), E4M3, dzi_mx, E5M2)
+            dw = sbuf([P, N], F32, "dw%d" % c, dw_at)
             nc.scalar.copy(dw[:], acc[:])
             nc.scalar.dma_start(out_1[block(c), :], dw[:])
 
-        e1_woven = turn_e(1, "four")
-        e0_woven = turn_e(0, "one2")
+        e_woven = {1: turn_e(1, "four"), 0: turn_e(0, "four", E_END)}
         scatter(0)
         scatter(1)
+        gather_e(3)
+        quantise_e(1)
+        quantise_e(0)
+        table_gradient(2, sbuf([P, N], F32, "de2", E_END - KIB)[:])
+        table_gradient(3, sbuf([P, N], F32, "de3", E_AT[3] + 2 * KIB)[:])
+        dzi_mx = mx_tiles(N, "dzi", E_AT[3] + 4 * KIB)
+        quantise(dzi_mx, everything, dz_i, E5M2)
         scatter(2)
         cast_e(2)
         gather_e(2)
-        e2_woven = turn_e(2, "one0")
-        gather_e(3)
-        table_gradient(3, sbuf([P, N], F32, "de3", E_AT[3])[:])
-        dzi_mx = mx_tiles(N, "dzi", E_AT[3] + 2 * KIB)
-        quantise(dzi_mx, everything, dz_i, E5M2)
-        e3_woven = turn_e(3, "four")
-        weight_gradient(0, e0_woven, "one0")
-        weight_gradient(1, e1_woven, "one0")
-        weight_gradient(2, e2_woven, "one1")
+        e_woven[2] = turn_e(2, "four")
+        e_woven[3] = turn_e(3, "one2")
+        weight_gradient(0, "one0", E_HALF_AT)
+        weight_gradient(1, "one1", E_HALF_AT + 2 * KIB)
+        quantise_e(3)
+        quantise_e(2)
+        weight_gradient(3, "one3")
+        weight_gradient(2, "four")
         scatter(3)
-        weight_gradient(3, e3_woven, "one3", E_AT[3])

@@ -20,6 +20,7 @@ HALF = N // 2
 ITEMS = 2048
 TILES = N // P
 WINDOWS = 3
+SEAM = 16
 E_ON_SCALAR = (0, 2)
 
 KIB = 1024
@@ -66,11 +67,6 @@ def tile_attend_gtower_sil_EW_kernel(tc, eT, W, xT, G, hT, cf, ts, offs, out_0, 
                 start=True,
                 stop=True,
             )
-
-        def turn_f32(src, turned, woven):
-            for j in range(PACK):
-                nc.tensor.transpose(turned[:, j, :], src[:, j:N:PACK], ident[:])
-            nc.scalar.copy(woven, turned.rearrange("s j m -> s m j"))
 
         def block(c):
             return slice(c * P, (c + 1) * P)
@@ -181,17 +177,24 @@ def tile_attend_gtower_sil_EW_kernel(tc, eT, W, xT, G, hT, cf, ts, offs, out_0, 
             nc.vector.tensor_copy(dz_f[a][:], dz_it[:, half(a), :])
 
         w_woven = [sbuf([P, HALF, PACK], BF16, "w_woven0"), sbuf([P, HALF, PACK], BF16, "w_woven1", E_AT[0])]
-        w_turned = psum([P, TILES, PACK, P], "w_turned", "four")
+        w_turned = psum([P, 2, 2, 2, P], "w_turned", "four")
         e_half = {}
 
         def cast_e(c):
             e_half[c] = sbuf([P, ITEMS], BF16, "e_half%d" % c, E_HALF_AT)
             nc.scalar.activation(e_half[c][:], e_win[c][:], ACT.Copy)
 
-        for c in range(TILES):
-            if c == 2:
+        for a in range(2):
+            w_half = sbuf([P, 2 * N], BF16, "w_half%d" % a)
+            nc.scalar.copy(w_half[:], w_raw[a][:].rearrange("p c f -> p (c f)"))
+            w_words = w_half[:].bitcast(F32).rearrange("p (c w) -> p c w", c=2)
+            for c in range(2):
+                for u in range(2):
+                    nc.tensor.transpose(w_turned[:, a, c, u, :], w_words[:, c, u:HALF:2], ident[:])
+            if a == 1:
                 cast_e(0)
-            turn_f32(w_raw[c // 2][:, c % 2, :], w_turned[:, c, :, :], w_woven[c // 2][:, block(c % 2), :])
+            w_woven_words = w_woven[a][:].rearrange("s d j -> s (d j)").bitcast(F32).rearrange("s (c m u) -> s c m u", c=2, u=2)
+            nc.scalar.copy(w_woven_words, w_turned[:, a, :, :, :].rearrange("s c u m -> s c m u"))
         w_mx = [mx_tiles(HALF, "w0", "slope3")]
         quantise(w_mx[0], half(0), w_woven[0], E4M3)
 
@@ -208,14 +211,12 @@ def tile_attend_gtower_sil_EW_kernel(tc, eT, W, xT, G, hT, cf, ts, offs, out_0, 
             else:
                 nc.vector.tensor_copy(e[c][:], e_win[c][:].indirect(offsets[:]))
 
-        def turn_e(c, bank, at=None):
+        def turn_e(c, bank, e_woven):
             e_words = e[c][:].bitcast(F32)
             turned = psum([P, 2, P], "e_turned%d" % c, bank)
             for u in range(2):
                 nc.tensor.transpose(turned[:, u, :], e_words[:, u:HALF:2], ident[:])
-            e_woven = sbuf([P, P, PACK], BF16, "e_woven%d" % c, at)
-            e_woven_words = e_woven[:].rearrange("s d r -> s (d r)").bitcast(F32).rearrange("s (d u) -> s d u", u=2)
-            nc.scalar.copy(e_woven_words, turned[:].rearrange("s u m -> s m u"))
+            nc.scalar.copy(e_woven.rearrange("s (d u) -> s d u", u=2), turned[:].rearrange("s u m -> s m u"))
             return e_woven
 
         de = {}
@@ -232,7 +233,7 @@ def tile_attend_gtower_sil_EW_kernel(tc, eT, W, xT, G, hT, cf, ts, offs, out_0, 
         table_gradient(1, de01[:, 1, :])
         w_mx.append(mx_tiles(HALF, "w1", E_AT[1] + 2 * KIB))
         quantise(w_mx[1], half(0), w_woven[1], E4M3)
-        gather_e(0, "slope3")
+        gather_e(0)
 
         dz_i = sbuf([P, N, PACK], BF16, "dz_i")
         dz_words = dz[:].bitcast(F32)
@@ -253,7 +254,7 @@ def tile_attend_gtower_sil_EW_kernel(tc, eT, W, xT, G, hT, cf, ts, offs, out_0, 
 
         def quantise_e(c):
             e_mx[c] = mx_tiles(P, "e%d" % c)
-            quantise(e_mx[c], block(0), e_woven[c], E4M3)
+            nc.vector.quantize_mx(out=e_mx[c][0][:].bitcast(E4M3), scales=e_mx[c][1][:], in_=e_woven[c].bitcast(BF16))
 
         def weight_gradient(c, bank, dw_at=None):
             acc = psum([P, N], "dw_acc%d" % c, bank)
@@ -262,25 +263,32 @@ def tile_attend_gtower_sil_EW_kernel(tc, eT, W, xT, G, hT, cf, ts, offs, out_0, 
             nc.scalar.copy(dw[:], acc[:])
             nc.scalar.dma_start(out_1[block(c), :], dw[:])
 
-        e_woven = {1: turn_e(1, "four"), 0: turn_e(0, "four", E_END)}
+        e_woven = {}
+        e_woven[1] = turn_e(1, "four", sbuf([P, HALF], F32, "e_woven1")[:])
+        e_woven[0] = turn_e(0, "four", sbuf([P, HALF], F32, "e_woven0", E_END)[:])
         scatter(0)
         scatter(1)
         gather_e(3)
         quantise_e(1)
         quantise_e(0)
         table_gradient(2, sbuf([P, N], F32, "de2", E_END - KIB)[:])
-        table_gradient(3, sbuf([P, N], F32, "de3", E_AT[3] + 2 * KIB)[:])
+        last = sbuf([P, N - SEAM + HALF], F32, "last", E_AT[3])
+        de[3] = last[:, :N]
+        last_acc = psum([P, N], "de_acc3", "one3")
+        multiply(last_acc[:], w_mx[1], block(1), E4M3, dzf_mx, E5M2)
+        nc.scalar.copy(last[:, : N - SEAM], last_acc[:, : N - SEAM])
         dzi_mx = mx_tiles(N, "dzi", E_AT[3] + 4 * KIB)
         quantise(dzi_mx, everything, dz_i, E5M2)
         scatter(2)
         cast_e(2)
         gather_e(2)
-        e_woven[2] = turn_e(2, "four")
-        e_woven[3] = turn_e(3, "one2")
+        e_woven[2] = turn_e(2, "four", last[:, N - SEAM :])
+        e_woven[3] = turn_e(3, "one2", sbuf([P, HALF], F32, "e_woven3")[:])
         weight_gradient(0, "one0", E_HALF_AT)
         weight_gradient(1, "one1", E_HALF_AT + 2 * KIB)
         quantise_e(3)
         quantise_e(2)
-        weight_gradient(3, "one3")
+        nc.vector.tensor_copy(last[:, N - SEAM : N], last_acc[:, N - SEAM :])
+        weight_gradient(3, "one2")
         weight_gradient(2, "four")
         scatter(3)

@@ -20,14 +20,13 @@ HALF = N // 2
 ITEMS = 2048
 TILES = N // P
 WINDOWS = 3
-SEAM = 16
-E_ON_SCALAR = (0, 2)
+E_ON_VECTOR = (1,)
 
 KIB = 1024
 H_AT = [0, 8 * KIB, 16 * KIB, 24 * KIB]
-E_AT = [32 * KIB, 40 * KIB, 48 * KIB, 56 * KIB]
-E_END = 64 * KIB
-E_HALF_AT = 66 * KIB
+E_AT = [32 * KIB, 42 * KIB, 50 * KIB, 58 * KIB]
+E_HALF_AT = {0: H_AT[3] + 4 * KIB, 2: 66 * KIB, 3: 70 * KIB}
+SIDE = ITEMS // 2
 
 FLOPS = 3 * 2 * N * N * N
 BYTES = 4 * (3 * N * ITEMS + 4 * N * N + ITEMS + N) + 2 * P * (N // 16)
@@ -46,16 +45,14 @@ def tile_attend_gtower_sil_EW_kernel(tc, eT, W, xT, G, hT, cf, ts, offs, out_0, 
                 return arena.tile(shape, dtype, name=name, align_bytes=64, offset=tag)
             return sb.tile(shape, dtype, name=name, tag=tag or name, align_bytes=64)
 
-        def psum(shape, name, tag):
-            return ps.tile(shape, F32, name=name, tag=tag)
+        def psum(shape, name, bank):
+            return ps.tile(shape, F32, name=name, tag="bank%d" % bank)
 
         def mx_tiles(width, name, tag=None):
             return sbuf([P, width], U32, name + "_codes", tag), sbuf([P, width], U8, name + "_scales")
 
         def quantise(mx, cols, woven, fmt):
-            nc.vector.quantize_mx(
-                out=mx[0][:, cols].bitcast(fmt), scales=mx[1][:, cols], in_=woven[:].rearrange("p c j -> p (c j)")
-            )
+            nc.vector.quantize_mx(out=mx[0][:, cols].bitcast(fmt), scales=mx[1][:, cols], in_=woven)
 
         def multiply(acc, still, still_cols, still_fmt, moving, moving_fmt):
             nc.tensor.matmul_mx(
@@ -68,45 +65,62 @@ def tile_attend_gtower_sil_EW_kernel(tc, eT, W, xT, G, hT, cf, ts, offs, out_0, 
                 stop=True,
             )
 
+        def weave(woven, planes):
+            nc.vector.tensor_copy(
+                woven[:].rearrange("p (c i) t -> p c t i", i=PACK), planes.rearrange("p t (c i) -> p c t i", i=PACK)
+            )
+
         def block(c):
             return slice(c * P, (c + 1) * P)
 
         def half(a):
             return slice(a * HALF, (a + 1) * HALF)
 
+        def side(a):
+            return slice(a * SIDE, (a + 1) * SIDE)
+
         everything = slice(0, N)
 
         offsets = lists.tile([P, N // 16], U16, name="offsets")
         nc.sync.dma_start(offsets[:], offs)
+
+        def listed(window, cols=everything):
+            return window[:].indirect(offsets[:, cols.start // 16 : cols.stop // 16])
 
         h_rows = hT.rearrange("(p t) n -> t p n", t=PACK)
         h_win = [sbuf([P, ITEMS], F32, "h_win%d" % t, H_AT[t]) for t in range(PACK)]
         x_rows = xT.rearrange("(p t) r -> t p r", t=PACK)
         x_raw = [sbuf([P, N], F32, "x_raw%d" % t) for t in range(PACK)]
         g_rows = G.rearrange("(p j) i -> p j i", j=PACK)
-        g_raw = [sbuf([P, PACK, HALF], F32, "g_raw%d" % a) for a in range(2)]
+        g_raw = sbuf([P, PACK, N], F32, "g_raw")
         w_rows = W.rearrange("(p a c) f -> a p c f", a=2, c=2)
         w_raw = [sbuf([P, 2, N], F32, "w_raw%d" % a) for a in range(2)]
         out_0_rows = out_0.rearrange("(p c) n -> c p n", c=TILES)
-        e_win = [sbuf([P, ITEMS], F32, "e_win%d" % c, E_AT[c]) for c in range(TILES)]
+        e_win = sbuf([P, ITEMS], F32, "e_win", E_AT[1])
+        e_sides = {
+            c: [sbuf([P, SIDE], F32, "e_side%d_%d" % (c, a), E_AT[c] + a * 4 * KIB) for a in range(2)] for c in range(TILES) if c not in E_ON_VECTOR
+        }
         ts_win = sbuf([P, ITEMS], F32, "ts_win")
         cf_col = sbuf([P, PACK], F32, "cf_col")
 
-        nc.vector.memset(ts_win[:], 0.0)
+        nc.gpsimd.memset(ts_win[:], 0.0)
         nc.sync.dma_start(h_win[0][:], h_rows[0])
         nc.sync.dma_start(ts_win[0:1, :], ts[0:1, :])
         nc.scalar.dma_start(cf_col[:], cf.rearrange("(p t) o -> p (t o)", t=PACK))
         for t in range(PACK):
             nc.sync.dma_start(x_raw[t][:], x_rows[t])
-        nc.sync.dma_start(g_raw[0][:], g_rows[:, :, half(0)])
+        nc.sync.dma_start(g_raw[:], g_rows)
         nc.sync.dma_start(h_win[1][:], h_rows[1])
-        nc.sync.dma_start(g_raw[1][:], g_rows[:, :, half(1)])
         nc.sync.dma_start(h_win[2][:], h_rows[2])
+        nc.sync.dma_start(w_raw[0][:], w_rows[0])
         nc.sync.dma_start(h_win[3][:], h_rows[3])
-        for a in range(2):
-            nc.sync.dma_start(w_raw[a][:], w_rows[a])
-        for c in range(TILES):
-            nc.sync.dma_start(e_win[c][:], eT[block(c), :])
+        nc.sync.dma_start(e_sides[0][0][:], eT[block(0), side(0)])
+        nc.sync.dma_start(w_raw[1][:], w_rows[1])
+        nc.sync.dma_start(e_sides[0][1][:], eT[block(0), side(1)])
+        nc.sync.dma_start(e_win[:], eT[block(1), :])
+        for c in range(2, TILES):
+            for a in range(2):
+                nc.sync.dma_start(e_sides[c][a][:], eT[block(c), side(a)])
 
         ident = sbuf([P, P], F32, "ident")
         make_identity(nc, ident[:])
@@ -114,181 +128,207 @@ def tile_attend_gtower_sil_EW_kernel(tc, eT, W, xT, G, hT, cf, ts, offs, out_0, 
         for window in windows:
             nc.gpsimd.memset(window[:], 0.0)
 
-        slope = [sbuf([P, N], F32, "slope%d" % t) for t in range(PACK)]
+        h = {}
+        s = [sbuf([P, N], F32, "s%d" % t) for t in range(PACK)]
+        slope = [sbuf([P, N], F32, "slope%d" % t, H_AT[2] if t == 1 else None) for t in range(PACK)]
 
-        def make_slope(t, h_tag=None, a_tag=None, s_tag=None):
-            h = sbuf([P, N], F32, "h%d" % t, h_tag)
-            nc.vector.tensor_copy(h[:], h_win[t][:].indirect(offsets[:]))
-            s = sbuf([P, N], F32, "s%d" % t, s_tag)
-            a = sbuf([P, N], F32, "a%d" % t, a_tag)
-            nc.scalar.activation(s[:], h[:], ACT.Sigmoid)
-            nc.vector.scalar_tensor_tensor(a[:], s[:], 1.0, h[:], ALU.subtract, ALU.mult)
-            nc.vector.scalar_tensor_tensor(slope[t][:], a[:], 1.0, s[:], ALU.subtract, ALU.mult)
+        def gather_h(t, pieces=(everything,), tag=None):
+            h[t] = sbuf([P, N], F32, "h%d" % t, tag)
+            for cols in pieces:
+                nc.vector.tensor_copy(h[t][:, cols], listed(h_win[t], cols))
+                nc.scalar.activation(s[t][:, cols], h[t][:, cols], ACT.Sigmoid)
 
-        make_slope(0)
+        part = [sbuf([P, N], F32, "part%d" % t) for t in range(PACK)]
+
+        def make_part(t, cols=everything):
+            nc.vector.scalar_tensor_tensor(part[t][:, cols], s[t][:, cols], 1.0, h[t][:, cols], ALU.subtract, ALU.mult)
+
+        def make_slope(t, cols=everything):
+            nc.vector.scalar_tensor_tensor(slope[t][:, cols], part[t][:, cols], 1.0, s[t][:, cols], ALU.subtract, ALU.mult)
+
+        gather_h(0)
 
         ts_row = sbuf([P, N], F32, "ts_row")
-        nc.vector.tensor_copy(ts_row[:], ts_win[:].indirect(offsets[:]))
+        nc.vector.tensor_copy(ts_row[:], listed(ts_win))
+        make_part(0)
+        make_slope(0)
 
-        x_woven = sbuf([P, N, PACK], BF16, "x_woven")
-        x_woven_words = x_woven[:].rearrange("s f r -> s (f r)").bitcast(F32).rearrange("s (t m u) -> s t m u", t=PACK, u=2)
+        x_woven = sbuf([P, N * PACK], BF16, "x_woven")
+        x_woven_words = x_woven[:].bitcast(F32).rearrange("s (t m u) -> s t m u", t=PACK, u=2)
         for t in range(PACK):
-            x_half = sbuf([P, N], BF16, "x_half%d" % t)
+            x_half = sbuf([P, N], BF16, "x_half%d" % t, H_AT[0] + t * KIB if t > 0 else None)
             nc.scalar.copy(x_half[:], x_raw[t][:])
             x_words = x_half[:].bitcast(F32)
-            turned = psum([P, 2, P], "x_turned%d" % t, "one%d" % t)
+            turned = psum([P, 2, P], "x_turned%d" % t, t)
             for u in range(2):
                 nc.tensor.transpose(turned[:, u, :], x_words[:, u:HALF:2], ident[:])
             nc.scalar.copy(x_woven_words[:, t, :, :], turned[:].rearrange("s u m -> s m u"))
-        ts_turned = psum([P, TILES, P], "ts_turned", "one2")
+        ts_turned = psum([P, TILES, P], "ts_turned", 7)
         for c in range(TILES):
             nc.tensor.transpose(ts_turned[:, c, :], ts_row[:, block(c)], ident[:])
         ts_col = sbuf([P, TILES], F32, "ts_col")
         nc.scalar.activation(ts_col[:], ts_turned[:, :, 0], ACT.Copy, scale=-1.0)
-        g_mx = mx_tiles(N, "g")
-        g_woven = [sbuf([P, HALF, PACK], BF16, "g_woven0", "h0"), sbuf([P, HALF, PACK], BF16, "g_woven1", H_AT[1])]
-        nc.vector.tensor_copy(g_woven[0][:], g_raw[0][:].rearrange("p j i -> p i j"))
-        quantise(g_mx, half(0), g_woven[0], E5M2)
-        x_mx = mx_tiles(N, "x", "h0")
-        quantise(x_mx, everything, x_woven, E4M3)
-        make_slope(1, "x_woven")
-        nc.vector.tensor_copy(g_woven[1][:], g_raw[1][:].rearrange("p j i -> p i j"))
-        quantise(g_mx, half(1), g_woven[1], E5M2)
-
-        dv_ts = [sbuf([P, N], F32, "dv_ts%d" % c) for c in range(TILES)]
-        dv_t = psum([P, TILES, N], "dv_t", "four")
-        for c in range(TILES):
-            multiply(dv_t[:, c, :], g_mx, block(c), E5M2, x_mx, E4M3)
-            nc.scalar.activation(dv_ts[c][:], dv_t[:, c, :], ACT.Copy, scale=ts_col[:, c : c + 1])
-        make_slope(2, H_AT[1], H_AT[3])
-        dv = [psum([P, N], "dv%d" % t, "one%d" % t) for t in range(PACK)]
-        for c in range(TILES):
-            for t in range(PACK):
-                nc.tensor.transpose(dv[t][:, block(c)], dv_ts[c][:, block(t)], ident[:])
-        make_slope(3, H_AT[2])
-
-        dz = sbuf([P, PACK, N], BF16, "dz", H_AT[2])
-        for t in range(PACK):
-            nc.vector.scalar_tensor_tensor(dz[:, t, :], dv[t][:], cf_col[:, t : t + 1], slope[t][:], ALU.mult, ALU.mult)
-
-        dz_f = [sbuf([P, HALF, PACK], BF16, "dz_f%d" % a) for a in range(2)]
-        dz_it = dz[:].rearrange("p t i -> p i t")
+        g_woven = [sbuf([P, HALF, PACK], BF16, "g_woven%d" % a, "h0" if a == 0 else None) for a in range(2)]
         for a in range(2):
-            nc.vector.tensor_copy(dz_f[a][:], dz_it[:, half(a), :])
+            weave(g_woven[a], g_raw[:, :, half(a)])
+        g_mx = [mx_tiles(HALF, "g0")]
+        quantise(g_mx[0], half(0), g_woven[0][:].rearrange("p i j -> p (i j)"), E5M2)
+        x_mx = mx_tiles(N, "x", "g_raw")
+        quantise(x_mx, everything, x_woven[:], E4M3)
+        gather_h(1, tag="x_woven")
+        g_mx.append(mx_tiles(HALF, "g1", H_AT[1] + 2 * KIB))
+        quantise(g_mx[1], half(0), g_woven[1][:].rearrange("p i j -> p (i j)"), E5M2)
 
-        w_woven = [sbuf([P, HALF, PACK], BF16, "w_woven0"), sbuf([P, HALF, PACK], BF16, "w_woven1", E_AT[0])]
-        w_turned = psum([P, 2, 2, 2, P], "w_turned", "four")
-        e_half = {}
+        dv_ts = [sbuf([P, N], F32, "dv_ts%d" % c, H_AT[1] if c == 0 else None) for c in range(TILES)]
+        dv = [psum([P, N], "dv%d" % t, t) for t in range(PACK)]
+        for c in range(TILES):
+            dv_t = psum([P, N], "dv_t%d" % c, 4 + c)
+            multiply(dv_t[:], g_mx[c // 2], block(c % 2), E5M2, x_mx, E4M3)
+            nc.scalar.activation(dv_ts[c][:], dv_t[:], ACT.Copy, scale=ts_col[:, c : c + 1])
+        for c, t in [(c, t) for c in range(2) for t in range(PACK)] + [(c, t) for t in range(PACK) for c in range(2, TILES)]:
+            nc.tensor.transpose(dv[t][:, block(c)], dv_ts[c][:, block(t)], ident[:])
 
-        def cast_e(c):
-            e_half[c] = sbuf([P, ITEMS], BF16, "e_half%d" % c, E_HALF_AT)
-            nc.scalar.activation(e_half[c][:], e_win[c][:], ACT.Copy)
+        w_woven = {}
 
-        for a in range(2):
-            w_half = sbuf([P, 2 * N], BF16, "w_half%d" % a)
+        w_turned = {}
+
+        def turn_w(a, bank, tag=None):
+            w_half = sbuf([P, 2 * N], BF16, "w_half%d" % a, tag)
             nc.scalar.copy(w_half[:], w_raw[a][:].rearrange("p c f -> p (c f)"))
             w_words = w_half[:].bitcast(F32).rearrange("p (c w) -> p c w", c=2)
+            w_turned[a] = psum([P, 2, 2, P], "w_turned%d" % a, bank)
             for c in range(2):
                 for u in range(2):
-                    nc.tensor.transpose(w_turned[:, a, c, u, :], w_words[:, c, u:HALF:2], ident[:])
-            if a == 1:
-                cast_e(0)
-            w_woven_words = w_woven[a][:].rearrange("s d j -> s (d j)").bitcast(F32).rearrange("s (c m u) -> s c m u", c=2, u=2)
-            nc.scalar.copy(w_woven_words, w_turned[:, a, :, :, :].rearrange("s c u m -> s c m u"))
-        w_mx = [mx_tiles(HALF, "w0", "slope3")]
-        quantise(w_mx[0], half(0), w_woven[0], E4M3)
+                    nc.tensor.transpose(w_turned[a][:, c, u, :], w_words[:, c, u:HALF:2], ident[:])
+
+        def weave_w(a, tag):
+            w_woven[a] = sbuf([P, HALF * PACK], BF16, "w_woven%d" % a, tag)
+            w_woven_words = w_woven[a][:].bitcast(F32).rearrange("s (c m u) -> s c m u", c=2, u=2)
+            nc.scalar.copy(w_woven_words, w_turned[a][:].rearrange("s c u m -> s c m u"))
+
+        e_half = {c: sbuf([P, ITEMS], BF16, "e_half%d" % c, E_HALF_AT[c]) for c in range(TILES) if c not in E_ON_VECTOR}
+
+        def cast_e(c, a):
+            nc.scalar.activation(e_half[c][:, side(a)], e_sides[c][a][:], ACT.Copy)
+
+        dz = sbuf([P, PACK * N], BF16, "dz", H_AT[3])
+
+        def make_dz(t, cols=everything):
+            nc.vector.scalar_tensor_tensor(
+                dz[:, t * N + cols.start : t * N + cols.stop], dv[t][:, cols], cf_col[:, t : t + 1], slope[t][:, cols], ALU.mult, ALU.mult
+            )
+
+        make_part(1)
+        gather_h(2, (half(0), half(1)))
+        turn_w(0, 4, H_AT[2] + 4 * KIB)
+        weave_w(0, None)
+        make_slope(1)
+        for a in range(2):
+            make_part(2, half(a))
+        gather_h(3, tag=H_AT[2] + 2 * KIB)
+        make_dz(0)
+        make_slope(2)
+        make_part(3)
+        make_dz(1)
+        make_slope(3)
+        make_dz(2)
+        make_dz(3)
+
+        cast_e(0, 0)
+        turn_w(1, 5, E_AT[0] + 2 * KIB)
+        cast_e(0, 1)
+        weave_w(1, E_AT[0] + 4 * KIB)
 
         dzf_mx = mx_tiles(N, "dzf")
+        dz_planes = dz[:].rearrange("p (t i) -> p t i", t=PACK)
+        dz_f = [sbuf([P, HALF, PACK], BF16, "dz_f%d" % a) for a in range(2)]
         for a in range(2):
-            quantise(dzf_mx, half(a), dz_f[a], E5M2)
+            weave(dz_f[a], dz_planes[:, :, half(a)])
+        w_mx = [mx_tiles(HALF, "w0", "slope3")]
+        quantise(w_mx[0], half(0), w_woven[0][:], E4M3)
+        for a in range(2):
+            quantise(dzf_mx, half(a), dz_f[a][:].rearrange("p i t -> p (i t)"), E5M2)
 
-        e = {}
-
-        def gather_e(c, tag=None):
-            e[c] = sbuf([P, N], BF16, "e%d" % c, tag)
-            if c in E_ON_SCALAR:
-                nc.scalar.activation(e[c][:], e_half[c][:].indirect(offsets[:]), ACT.Copy)
-            else:
-                nc.vector.tensor_copy(e[c][:], e_win[c][:].indirect(offsets[:]))
-
-        def turn_e(c, bank, e_woven):
-            e_words = e[c][:].bitcast(F32)
-            turned = psum([P, 2, P], "e_turned%d" % c, bank)
-            for u in range(2):
-                nc.tensor.transpose(turned[:, u, :], e_words[:, u:HALF:2], ident[:])
-            nc.scalar.copy(e_woven.rearrange("s (d u) -> s d u", u=2), turned[:].rearrange("s u m -> s m u"))
-            return e_woven
-
-        de = {}
-
-        def table_gradient(c, target):
-            de_acc = psum([P, N], "de_acc%d" % c, "one%d" % c)
-            multiply(de_acc[:], w_mx[c // 2], block(c % 2), E4M3, dzf_mx, E5M2)
-            de[c] = target
-            nc.scalar.copy(target, de_acc[:])
-
-        gather_e(1, "dz_f1")
-        de01 = sbuf([P, 2, N], F32, "de01", E_AT[1] - 2 * KIB)
-        table_gradient(0, de01[:, 0, :])
-        table_gradient(1, de01[:, 1, :])
-        w_mx.append(mx_tiles(HALF, "w1", E_AT[1] + 2 * KIB))
-        quantise(w_mx[1], half(0), w_woven[1], E4M3)
-        gather_e(0)
-
-        dz_i = sbuf([P, N, PACK], BF16, "dz_i")
-        dz_words = dz[:].bitcast(F32)
-        dz_i_words = dz_i[:].rearrange("s f r -> s (f r)").bitcast(F32).rearrange("s (p t u) -> s p t u", t=PACK, u=2)
+        dz_i = sbuf([P, N * PACK], BF16, "dz_i", E_AT[0] + 6 * KIB)
+        dz_words = dz[:].bitcast(F32).rearrange("p (t w) -> p t w", t=PACK)
+        dz_i_words = dz_i[:].bitcast(F32).rearrange("s (p t u) -> s p t u", t=PACK, u=2)
         for b in range(2):
-            turned = psum([P, 2, 2, P], "dz_turned%d" % b, "one%d" % b)
+            turned = psum([P, 2, 2, P], "dz_turned%d" % b, b)
             for t in range(2):
                 for u in range(2):
                     nc.tensor.transpose(turned[:, t, u, :], dz_words[:, 2 * b + t, u:HALF:2], ident[:])
             nc.scalar.copy(dz_i_words[:, :, 2 * b : 2 * b + 2, :], turned[:].rearrange("s t u p -> s p t u"))
 
+        e = {}
+
+        def gather_e(c, tag=None):
+            e[c] = sbuf([P, N], BF16, "e%d" % c, tag)
+            if c in E_ON_VECTOR:
+                nc.vector.tensor_copy(e[c][:], listed(e_win))
+            else:
+                nc.scalar.activation(e[c][:], listed(e_half[c]), ACT.Copy)
+
+        e_woven = sbuf([P, TILES * HALF], F32, "e_woven")
+
+        def turn_e(c, bank):
+            e_words = e[c][:].bitcast(F32)
+            turned = psum([P, 2, P], "e_turned%d" % c, bank)
+            for u in range(2):
+                nc.tensor.transpose(turned[:, u, :], e_words[:, u:HALF:2], ident[:])
+            nc.scalar.copy(e_woven[:, half(c)].rearrange("s (d u) -> s d u", u=2), turned[:].rearrange("s u m -> s m u"))
+
+        de = {}
+
+        def table_gradient(c, bank, tag=None):
+            de_acc = psum([P, N], "de_acc%d" % c, bank)
+            multiply(de_acc[:], w_mx[c // 2], block(c % 2), E4M3, dzf_mx, E5M2)
+            de[c] = sbuf([P, N], F32, "de%d" % c, tag)
+            nc.scalar.copy(de[c][:], de_acc[:])
+
         def scatter(c):
             window = windows[c % WINDOWS]
-            nc.vector.tensor_copy(window[:].indirect(offsets[:]), de[c])
+            nc.vector.tensor_copy(listed(window), de[c][:])
             nc.sync.dma_start(out_0_rows[c], window[:])
 
-        e_mx = {}
+        def quantise_e(first, end):
+            quantise(e_mx, slice(first * P, end * P), e_woven[:, first * HALF : end * HALF].bitcast(BF16), E4M3)
 
-        def quantise_e(c):
-            e_mx[c] = mx_tiles(P, "e%d" % c)
-            nc.vector.quantize_mx(out=e_mx[c][0][:].bitcast(E4M3), scales=e_mx[c][1][:], in_=e_woven[c].bitcast(BF16))
-
-        def weight_gradient(c, bank, dw_at=None):
+        def weight_gradient(c, bank, tag):
             acc = psum([P, N], "dw_acc%d" % c, bank)
-            multiply(acc[:], e_mx[c], block(0), E4M3, dzi_mx, E5M2)
-            dw = sbuf([P, N], F32, "dw%d" % c, dw_at)
+            multiply(acc[:], e_mx, block(c), E4M3, dzi_mx, E5M2)
+            dw = sbuf([P, N], F32, "dw%d" % c, tag)
             nc.scalar.copy(dw[:], acc[:])
             nc.scalar.dma_start(out_1[block(c), :], dw[:])
 
-        e_woven = {}
-        e_woven[1] = turn_e(1, "four", sbuf([P, HALF], F32, "e_woven1")[:])
-        e_woven[0] = turn_e(0, "four", sbuf([P, HALF], F32, "e_woven0", E_END)[:])
+        gather_e(0, H_AT[3])
+        gather_e(1, "dz_f1")
+        table_gradient(0, 6, E_AT[1])
+        table_gradient(1, 7, H_AT[0])
+        w_mx.append(mx_tiles(HALF, "w1", E_AT[1] + 2 * KIB))
+        quantise(w_mx[1], half(0), w_woven[1][:], E4M3)
         scatter(0)
+        dzi_mx = mx_tiles(N, "dzi", E_AT[1] + 4 * KIB)
+        quantise(dzi_mx, everything, dz_i[:], E5M2)
         scatter(1)
-        gather_e(3)
-        quantise_e(1)
-        quantise_e(0)
-        table_gradient(2, sbuf([P, N], F32, "de2", E_END - KIB)[:])
-        last = sbuf([P, N - SEAM + HALF], F32, "last", E_AT[3])
-        de[3] = last[:, :N]
-        last_acc = psum([P, N], "de_acc3", "one3")
-        multiply(last_acc[:], w_mx[1], block(1), E4M3, dzf_mx, E5M2)
-        nc.scalar.copy(last[:, : N - SEAM], last_acc[:, : N - SEAM])
-        dzi_mx = mx_tiles(N, "dzi", E_AT[3] + 4 * KIB)
-        quantise(dzi_mx, everything, dz_i, E5M2)
-        scatter(2)
-        cast_e(2)
+        turn_e(0, 6)
+        turn_e(1, 7)
+        for a in range(2):
+            cast_e(2, a)
         gather_e(2)
-        e_woven[2] = turn_e(2, "four", last[:, N - SEAM :])
-        e_woven[3] = turn_e(3, "one2", sbuf([P, HALF], F32, "e_woven3")[:])
-        weight_gradient(0, "one0", E_HALF_AT)
-        weight_gradient(1, "one1", E_HALF_AT + 2 * KIB)
-        quantise_e(3)
-        quantise_e(2)
-        nc.vector.tensor_copy(last[:, N - SEAM : N], last_acc[:, N - SEAM :])
-        weight_gradient(3, "one2")
-        weight_gradient(2, "four")
+        e_mx = mx_tiles(N, "e", E_HALF_AT[2])
+        quantise_e(0, 2)
+        table_gradient(2, 3, E_HALF_AT[2] + 2 * KIB)
+        scatter(2)
+        turn_e(2, 2)
+        for a in range(2):
+            cast_e(3, a)
+        weight_gradient(0, 6, E_AT[3] + 4 * KIB)
+        weight_gradient(1, 7, E_AT[3] + 6 * KIB)
+        quantise_e(2, 3)
+        table_gradient(3, 2, H_AT[0] + 4 * KIB)
+        gather_e(3)
         scatter(3)
+        weight_gradient(2, 0, E_HALF_AT[3])
+        turn_e(3, 4)
+        quantise_e(3, 4)
+        weight_gradient(3, 1, None)

@@ -25,7 +25,7 @@ E_ON_VECTOR = (1,)
 KIB = 1024
 H_AT = [0, 8 * KIB, 16 * KIB, 24 * KIB]
 E_AT = [32 * KIB, 42 * KIB, 50 * KIB, 58 * KIB]
-E_HALF_AT = {0: H_AT[3] + 4 * KIB, 2: 66 * KIB, 3: 70 * KIB}
+E_HALF_AT = {0: 74 * KIB, 2: 66 * KIB, 3: 70 * KIB}
 SIDE = ITEMS // 2
 
 FLOPS = 3 * 2 * N * N * N
@@ -82,7 +82,6 @@ def tile_attend_gtower_sil_EW_kernel(tc, eT, W, xT, G, hT, cf, ts, offs, out_0, 
         everything = slice(0, N)
 
         offsets = lists.tile([P, N // 16], U16, name="offsets")
-        nc.sync.dma_start(offsets[:], offs)
 
         def listed(window, cols=everything):
             return window[:].indirect(offsets[:, cols.start // 16 : cols.stop // 16])
@@ -105,15 +104,16 @@ def tile_attend_gtower_sil_EW_kernel(tc, eT, W, xT, G, hT, cf, ts, offs, out_0, 
 
         nc.gpsimd.memset(ts_win[:], 0.0)
         nc.sync.dma_start(h_win[0][:], h_rows[0])
+        nc.sync.dma_start(offsets[:], offs)
         nc.sync.dma_start(ts_win[0:1, :], ts[0:1, :])
-        nc.scalar.dma_start(cf_col[:], cf.rearrange("(p t) o -> p (t o)", t=PACK))
         for t in range(PACK):
             nc.sync.dma_start(x_raw[t][:], x_rows[t])
         nc.sync.dma_start(g_raw[:], g_rows)
         nc.sync.dma_start(h_win[1][:], h_rows[1])
         nc.sync.dma_start(h_win[2][:], h_rows[2])
-        nc.sync.dma_start(w_raw[0][:], w_rows[0])
         nc.sync.dma_start(h_win[3][:], h_rows[3])
+        nc.sync.dma_start(cf_col[:], cf.rearrange("(p t) o -> p (t o)", t=PACK))
+        nc.sync.dma_start(w_raw[0][:], w_rows[0])
         nc.sync.dma_start(e_sides[0][0][:], eT[block(0), side(0)])
         nc.sync.dma_start(w_raw[1][:], w_rows[1])
         nc.sync.dma_start(e_sides[0][1][:], eT[block(0), side(1)])
@@ -220,8 +220,6 @@ def tile_attend_gtower_sil_EW_kernel(tc, eT, W, xT, G, hT, cf, ts, offs, out_0, 
 
         make_part(1)
         gather_h(2, (half(0), half(1)))
-        turn_w(0, 4, H_AT[2] + 4 * KIB)
-        weave_w(0, None)
         make_slope(1)
         for a in range(2):
             make_part(2, half(a))
@@ -234,7 +232,9 @@ def tile_attend_gtower_sil_EW_kernel(tc, eT, W, xT, G, hT, cf, ts, offs, out_0, 
         make_dz(2)
         make_dz(3)
 
+        turn_w(0, 4, H_AT[3] + 4 * KIB)
         cast_e(0, 0)
+        weave_w(0, E_AT[0])
         turn_w(1, 5, E_AT[0] + 2 * KIB)
         cast_e(0, 1)
         weave_w(1, E_AT[0] + 4 * KIB)
@@ -300,7 +300,6 @@ def tile_attend_gtower_sil_EW_kernel(tc, eT, W, xT, G, hT, cf, ts, offs, out_0, 
             nc.scalar.copy(dw[:], acc[:])
             nc.scalar.dma_start(out_1[block(c), :], dw[:])
 
-        gather_e(0, H_AT[3])
         gather_e(1, "dz_f1")
         table_gradient(0, 6, E_AT[1])
         table_gradient(1, 7, H_AT[0])
@@ -310,8 +309,9 @@ def tile_attend_gtower_sil_EW_kernel(tc, eT, W, xT, G, hT, cf, ts, offs, out_0, 
         dzi_mx = mx_tiles(N, "dzi", E_AT[1] + 4 * KIB)
         quantise(dzi_mx, everything, dz_i[:], E5M2)
         scatter(1)
-        turn_e(0, 6)
-        turn_e(1, 7)
+        turn_e(1, 6)
+        gather_e(0, "dz_f1")
+        turn_e(0, 7)
         for a in range(2):
             cast_e(2, a)
         gather_e(2)

@@ -93,7 +93,8 @@ def tile_attend_gtower_sil_EW_kernel(tc, eT, W, xT, G, hT, cf, ts, offs, out_0, 
         g_rows = G.rearrange("(p j) i -> p j i", j=PACK)
         g_raw = sbuf([P, PACK, N], F32, "g_raw")
         w_rows = W.rearrange("(p a c) f -> a p c f", a=2, c=2)
-        w_raw = [sbuf([P, 2, N], F32, "w_raw%d" % a) for a in range(2)]
+        w_first = [sbuf([P, N], F32, "w_first%d" % c) for c in range(2)]
+        w_second = sbuf([P, 2, N], F32, "w_second")
         out_0_rows = out_0.rearrange("(p c) n -> c p n", c=TILES)
         e_win = sbuf([P, ITEMS], F32, "e_win", E_AT[1])
         e_sides = {
@@ -112,10 +113,11 @@ def tile_attend_gtower_sil_EW_kernel(tc, eT, W, xT, G, hT, cf, ts, offs, out_0, 
         nc.sync.dma_start(h_win[1][:], h_rows[1])
         nc.sync.dma_start(h_win[2][:], h_rows[2])
         nc.sync.dma_start(h_win[3][:], h_rows[3])
+        nc.sync.dma_start(w_first[0][:], w_rows[0][:, 0, :])
         nc.sync.dma_start(cf_col[:], cf.rearrange("(p t) o -> p (t o)", t=PACK))
-        nc.sync.dma_start(w_raw[0][:], w_rows[0])
+        nc.sync.dma_start(w_first[1][:], w_rows[0][:, 1, :])
         nc.sync.dma_start(e_sides[0][0][:], eT[block(0), side(0)])
-        nc.sync.dma_start(w_raw[1][:], w_rows[1])
+        nc.sync.dma_start(w_second[:], w_rows[1])
         nc.sync.dma_start(e_sides[0][1][:], eT[block(0), side(1)])
         nc.sync.dma_start(e_win[:], eT[block(1), :])
         for c in range(2, TILES):
@@ -129,10 +131,11 @@ def tile_attend_gtower_sil_EW_kernel(tc, eT, W, xT, G, hT, cf, ts, offs, out_0, 
             nc.gpsimd.memset(window[:], 0.0)
 
         h = {}
-        s = [sbuf([P, N], F32, "s%d" % t) for t in range(PACK)]
+        s = {}
         slope = [sbuf([P, N], F32, "slope%d" % t, H_AT[2] if t == 1 else None) for t in range(PACK)]
 
-        def gather_h(t, pieces=(everything,), tag=None):
+        def gather_h(t, pieces=(everything,), tag=None, s_tag=None):
+            s[t] = sbuf([P, N], F32, "s%d" % t, s_tag)
             h[t] = sbuf([P, N], F32, "h%d" % t, tag)
             for cols in pieces:
                 nc.vector.tensor_copy(h[t][:, cols], listed(h_win[t], cols))
@@ -175,7 +178,7 @@ def tile_attend_gtower_sil_EW_kernel(tc, eT, W, xT, G, hT, cf, ts, offs, out_0, 
         quantise(g_mx[0], half(0), g_woven[0][:].rearrange("p i j -> p (i j)"), E5M2)
         x_mx = mx_tiles(N, "x", "g_raw")
         quantise(x_mx, everything, x_woven[:], E4M3)
-        gather_h(1, tag="x_woven")
+        gather_h(1, (half(0), half(1)), "x_woven")
         g_mx.append(mx_tiles(HALF, "g1", H_AT[1] + 2 * KIB))
         quantise(g_mx[1], half(0), g_woven[1][:].rearrange("p i j -> p (i j)"), E5M2)
 
@@ -190,16 +193,16 @@ def tile_attend_gtower_sil_EW_kernel(tc, eT, W, xT, G, hT, cf, ts, offs, out_0, 
 
         w_woven = {}
 
-        w_turned = {}
+        w_turned = [psum([P, 2, 2, P], "w_turned%d" % a, 4 + a) for a in range(2)]
 
-        def turn_w(a, bank, tag=None):
-            w_half = sbuf([P, 2 * N], BF16, "w_half%d" % a, tag)
-            nc.scalar.copy(w_half[:], w_raw[a][:].rearrange("p c f -> p (c f)"))
-            w_words = w_half[:].bitcast(F32).rearrange("p (c w) -> p c w", c=2)
-            w_turned[a] = psum([P, 2, 2, P], "w_turned%d" % a, bank)
-            for c in range(2):
+        def turn_w(first, end, rows, tag=None):
+            w_half = sbuf([P, (end - first) * N], BF16, "w_half%d" % first, tag)
+            nc.scalar.copy(w_half[:], rows)
+            w_words = w_half[:].bitcast(F32)
+            for c in range(first, end):
                 for u in range(2):
-                    nc.tensor.transpose(w_turned[a][:, c, u, :], w_words[:, c, u:HALF:2], ident[:])
+                    words = slice((c - first) * HALF + u, (c - first + 1) * HALF, 2)
+                    nc.tensor.transpose(w_turned[c // 2][:, c % 2, u, :], w_words[:, words], ident[:])
 
         def weave_w(a, tag):
             w_woven[a] = sbuf([P, HALF * PACK], BF16, "w_woven%d" % a, tag)
@@ -211,31 +214,35 @@ def tile_attend_gtower_sil_EW_kernel(tc, eT, W, xT, G, hT, cf, ts, offs, out_0, 
         def cast_e(c, a):
             nc.scalar.activation(e_half[c][:, side(a)], e_sides[c][a][:], ACT.Copy)
 
-        dz = sbuf([P, PACK * N], BF16, "dz", H_AT[3])
+        dz = sbuf([P, PACK * N], BF16, "dz", "part1")
 
         def make_dz(t, cols=everything):
             nc.vector.scalar_tensor_tensor(
                 dz[:, t * N + cols.start : t * N + cols.stop], dv[t][:, cols], cf_col[:, t : t + 1], slope[t][:, cols], ALU.mult, ALU.mult
             )
 
-        make_part(1)
+        for a in range(2):
+            make_part(1, half(a))
         gather_h(2, (half(0), half(1)))
         make_slope(1)
         for a in range(2):
             make_part(2, half(a))
-        gather_h(3, tag=H_AT[2] + 2 * KIB)
         make_dz(0)
         make_slope(2)
-        make_part(3)
+        turn_w(0, 1, w_first[0][:], H_AT[2] + 4 * KIB)
+        gather_h(3, (half(0), half(1)), H_AT[2] + 2 * KIB, "w_first0")
         make_dz(1)
-        make_slope(3)
+        for a in range(2):
+            make_part(3, half(a))
         make_dz(2)
-        make_dz(3)
+        for step in (make_slope, make_dz):
+            for a in range(2):
+                step(3, half(a))
 
-        turn_w(0, 4, H_AT[3] + 4 * KIB)
+        turn_w(1, 2, w_first[1][:], H_AT[3] + 4 * KIB)
         cast_e(0, 0)
         weave_w(0, E_AT[0])
-        turn_w(1, 5, E_AT[0] + 2 * KIB)
+        turn_w(2, 4, w_second[:].rearrange("p c f -> p (c f)"), E_AT[0] + 2 * KIB)
         cast_e(0, 1)
         weave_w(1, E_AT[0] + 4 * KIB)
 
@@ -300,9 +307,9 @@ def tile_attend_gtower_sil_EW_kernel(tc, eT, W, xT, G, hT, cf, ts, offs, out_0, 
             nc.scalar.copy(dw[:], acc[:])
             nc.scalar.dma_start(out_1[block(c), :], dw[:])
 
-        gather_e(1, "dz_f1")
+        gather_e(1, "dz_f0")
         table_gradient(0, 6, E_AT[1])
-        table_gradient(1, 7, H_AT[0])
+        table_gradient(1, 7, E_AT[1] + 6 * KIB)
         w_mx.append(mx_tiles(HALF, "w1", E_AT[1] + 2 * KIB))
         quantise(w_mx[1], half(0), w_woven[1][:], E4M3)
         scatter(0)
@@ -310,7 +317,7 @@ def tile_attend_gtower_sil_EW_kernel(tc, eT, W, xT, G, hT, cf, ts, offs, out_0, 
         quantise(dzi_mx, everything, dz_i[:], E5M2)
         scatter(1)
         turn_e(1, 6)
-        gather_e(0, "dz_f1")
+        gather_e(0, "dz_f0")
         turn_e(0, 7)
         for a in range(2):
             cast_e(2, a)

@@ -88,8 +88,8 @@ def tile_attend_gtower_sil_EW_kernel(tc, eT, W, xT, G, hT, cf, ts, offs, out_0, 
 
         h_rows = hT.rearrange("(p t) n -> t p n", t=PACK)
         h_win = [sbuf([P, ITEMS], F32, "h_win%d" % t, H_AT[t]) for t in range(PACK)]
-        x_rows = xT.rearrange("(p t) r -> t p r", t=PACK)
-        x_raw = [sbuf([P, N], F32, "x_raw%d" % t) for t in range(PACK)]
+        x_rows = xT.rearrange("(p a c) r -> a p c r", a=2, c=2)
+        x_raw = [sbuf([P, 2, N], F32, "x_raw%d" % a) for a in range(2)]
         g_rows = G.rearrange("(p j) i -> p j i", j=PACK)
         g_raw = sbuf([P, PACK, N], F32, "g_raw")
         w_rows = W.rearrange("(p a c) f -> a p c f", a=2, c=2)
@@ -107,8 +107,8 @@ def tile_attend_gtower_sil_EW_kernel(tc, eT, W, xT, G, hT, cf, ts, offs, out_0, 
         nc.sync.dma_start(h_win[0][:], h_rows[0])
         nc.sync.dma_start(offsets[:], offs)
         nc.sync.dma_start(ts_win[0:1, :], ts[0:1, :])
-        for t in range(PACK):
-            nc.sync.dma_start(x_raw[t][:], x_rows[t])
+        for a in range(2):
+            nc.sync.dma_start(x_raw[a][:], x_rows[a])
         nc.sync.dma_start(g_raw[:], g_rows)
         nc.sync.dma_start(h_win[1][:], h_rows[1])
         nc.sync.dma_start(h_win[2][:], h_rows[2])
@@ -126,9 +126,13 @@ def tile_attend_gtower_sil_EW_kernel(tc, eT, W, xT, G, hT, cf, ts, offs, out_0, 
 
         ident = sbuf([P, P], F32, "ident")
         make_identity(nc, ident[:])
-        windows = [sbuf([P, ITEMS], F32, "window%d" % w) for w in range(WINDOWS)]
-        for window in windows:
-            nc.gpsimd.memset(window[:], 0.0)
+        windows = []
+
+        def clear_window(tag=None):
+            windows.append(sbuf([P, ITEMS], F32, "window%d" % len(windows), tag))
+            nc.gpsimd.memset(windows[-1][:], 0.0)
+
+        clear_window()
 
         h = {}
         s = {}
@@ -160,7 +164,7 @@ def tile_attend_gtower_sil_EW_kernel(tc, eT, W, xT, G, hT, cf, ts, offs, out_0, 
         x_woven_words = x_woven[:].bitcast(F32).rearrange("s (t m u) -> s t m u", t=PACK, u=2)
         for t in range(PACK):
             x_half = sbuf([P, N], BF16, "x_half%d" % t, H_AT[0] + t * KIB if t > 0 else None)
-            nc.scalar.copy(x_half[:], x_raw[t][:])
+            nc.scalar.copy(x_half[:], x_raw[t // 2][:, t % 2, :])
             x_words = x_half[:].bitcast(F32)
             turned = psum([P, 2, P], "x_turned%d" % t, t)
             for u in range(2):
@@ -181,6 +185,8 @@ def tile_attend_gtower_sil_EW_kernel(tc, eT, W, xT, G, hT, cf, ts, offs, out_0, 
         gather_h(1, (half(0), half(1)), "x_woven")
         g_mx.append(mx_tiles(HALF, "g1", H_AT[1] + 2 * KIB))
         quantise(g_mx[1], half(0), g_woven[1][:].rearrange("p i j -> p (i j)"), E5M2)
+
+        clear_window("g_woven1")
 
         dv_ts = [sbuf([P, N], F32, "dv_ts%d" % c, H_AT[1] if c == 0 else None) for c in range(TILES)]
         dv = [psum([P, N], "dv%d" % t, t) for t in range(PACK)]
@@ -223,6 +229,7 @@ def tile_attend_gtower_sil_EW_kernel(tc, eT, W, xT, G, hT, cf, ts, offs, out_0, 
 
         for a in range(2):
             make_part(1, half(a))
+        clear_window("x_woven")
         gather_h(2, (half(0), half(1)))
         make_slope(1)
         for a in range(2):

@@ -26,6 +26,8 @@ KIB = 1024
 H_AT = [0, 8 * KIB, 16 * KIB, 24 * KIB]
 E_AT = [32 * KIB, 42 * KIB, 50 * KIB, 58 * KIB]
 E_HALF_AT = {0: 74 * KIB, 2: 66 * KIB, 3: 70 * KIB}
+E_LAST_AT = 80 * KIB
+LAP = 64
 SIDE = ITEMS // 2
 
 FLOPS = 3 * 2 * N * N * N
@@ -197,23 +199,13 @@ def tile_attend_gtower_sil_EW_kernel(tc, eT, W, xT, G, hT, cf, ts, offs, out_0, 
         for c, t in [(c, t) for c in range(2) for t in range(PACK)] + [(c, t) for t in range(PACK) for c in range(2, TILES)]:
             nc.tensor.transpose(dv[t][:, block(c)], dv_ts[c][:, block(t)], ident[:])
 
-        w_woven = {}
+        w_woven = [sbuf([P, HALF, PACK], BF16, "w_woven%d" % a, at) for a, at in enumerate((None, E_AT[0] + 4 * KIB))]
 
-        w_turned = [psum([P, 2, 2, P], "w_turned%d" % a, 4 + a) for a in range(2)]
-
-        def turn_w(first, end, rows, tag=None):
-            w_half = sbuf([P, (end - first) * N], BF16, "w_half%d" % first, tag)
-            nc.scalar.copy(w_half[:], rows)
-            w_words = w_half[:].bitcast(F32)
-            for c in range(first, end):
-                for u in range(2):
-                    words = slice((c - first) * HALF + u, (c - first + 1) * HALF, 2)
-                    nc.tensor.transpose(w_turned[c // 2][:, c % 2, u, :], w_words[:, words], ident[:])
-
-        def weave_w(a, tag):
-            w_woven[a] = sbuf([P, HALF * PACK], BF16, "w_woven%d" % a, tag)
-            w_woven_words = w_woven[a][:].bitcast(F32).rearrange("s (c m u) -> s c m u", c=2, u=2)
-            nc.scalar.copy(w_woven_words, w_turned[a][:].rearrange("s c u m -> s c m u"))
+        def turn_w(c, rows):
+            turned = psum([P, PACK, P], "w_turned%d" % c, 4 + c)
+            for t in range(PACK):
+                nc.tensor.transpose(turned[:, t, :], rows[:, t:N:PACK], ident[:])
+            nc.scalar.copy(w_woven[c // 2][:, block(c % 2), :], turned[:].rearrange("s t m -> s m t"))
 
         e_half = {c: sbuf([P, ITEMS], BF16, "e_half%d" % c, E_HALF_AT[c]) for c in range(TILES) if c not in E_ON_VECTOR}
 
@@ -236,8 +228,9 @@ def tile_attend_gtower_sil_EW_kernel(tc, eT, W, xT, G, hT, cf, ts, offs, out_0, 
             make_part(2, half(a))
         make_dz(0)
         make_slope(2)
-        turn_w(0, 1, w_first[0][:], H_AT[2] + 4 * KIB)
-        gather_h(3, (half(0), half(1)), H_AT[2] + 2 * KIB, "w_first0")
+        for c in range(2):
+            turn_w(c, w_first[c][:])
+        gather_h(3, (half(0), half(1)), H_AT[2] + 2 * KIB, "w_first1")
         make_dz(1)
         for a in range(2):
             make_part(3, half(a))
@@ -246,12 +239,10 @@ def tile_attend_gtower_sil_EW_kernel(tc, eT, W, xT, G, hT, cf, ts, offs, out_0, 
             for a in range(2):
                 step(3, half(a))
 
-        turn_w(1, 2, w_first[1][:], H_AT[3] + 4 * KIB)
-        cast_e(0, 0)
-        weave_w(0, E_AT[0])
-        turn_w(2, 4, w_second[:].rearrange("p c f -> p (c f)"), E_AT[0] + 2 * KIB)
-        cast_e(0, 1)
-        weave_w(1, E_AT[0] + 4 * KIB)
+        for a in range(2):
+            cast_e(0, a)
+        for c in range(2, TILES):
+            turn_w(c, w_second[:, c - 2, :])
 
         dzf_mx = mx_tiles(N, "dzf")
         dz_planes = dz[:].rearrange("p (t i) -> p t i", t=PACK)
@@ -259,7 +250,7 @@ def tile_attend_gtower_sil_EW_kernel(tc, eT, W, xT, G, hT, cf, ts, offs, out_0, 
         for a in range(2):
             weave(dz_f[a], dz_planes[:, :, half(a)])
         w_mx = [mx_tiles(HALF, "w0", "slope3")]
-        quantise(w_mx[0], half(0), w_woven[0][:], E4M3)
+        quantise(w_mx[0], half(0), w_woven[0][:].rearrange("s m t -> s (m t)"), E4M3)
         for a in range(2):
             quantise(dzf_mx, half(a), dz_f[a][:].rearrange("p i t -> p (i t)"), E5M2)
 
@@ -314,35 +305,34 @@ def tile_attend_gtower_sil_EW_kernel(tc, eT, W, xT, G, hT, cf, ts, offs, out_0, 
             nc.scalar.copy(dw[:], acc[:])
             nc.scalar.dma_start(out_1[block(c), :], dw[:])
 
+        gather_e(0)
         gather_e(1, "dz_f0")
-        table_gradient(0, 6, E_AT[1])
-        table_gradient(1, 7, E_AT[1] + 6 * KIB)
+        table_gradient(0, 2, E_AT[1])
+        table_gradient(1, 3, E_AT[1] + 6 * KIB)
         w_mx.append(mx_tiles(HALF, "w1", E_AT[1] + 2 * KIB))
-        quantise(w_mx[1], half(0), w_woven[1][:], E4M3)
-        scatter(0)
+        quantise(w_mx[1], half(0), w_woven[1][:].rearrange("s m t -> s (m t)"), E4M3)
         dzi_mx = mx_tiles(N, "dzi", E_AT[1] + 4 * KIB)
         quantise(dzi_mx, everything, dz_i[:], E5M2)
+        scatter(0)
         scatter(1)
-        turn_e(1, 6)
-        gather_e(0, "dz_f0")
-        turn_e(0, 7)
+        turn_e(0, 2)
+        turn_e(1, 3)
         for a in range(2):
             cast_e(2, a)
         gather_e(2)
         e_mx = mx_tiles(N, "e", E_HALF_AT[2])
         quantise_e(0, 2)
-        table_gradient(2, 3, E_HALF_AT[2] + 2 * KIB)
+        table_gradient(2, 5, E_HALF_AT[2] + 2 * KIB)
         scatter(2)
-        turn_e(2, 2)
+        turn_e(2, 4)
         for a in range(2):
             cast_e(3, a)
-        weight_gradient(0, 6, E_AT[3] + 4 * KIB)
-        weight_gradient(1, 7, E_AT[3] + 6 * KIB)
-        quantise_e(2, 3)
-        table_gradient(3, 2, H_AT[0] + 4 * KIB)
-        gather_e(3)
+        gather_e(3, E_LAST_AT)
+        weight_gradient(0, 0, E_HALF_AT[3])
+        turn_e(3, 7)
+        table_gradient(3, 6, E_LAST_AT - 2 * KIB + LAP)
+        quantise_e(2, 4)
         scatter(3)
-        weight_gradient(2, 0, E_HALF_AT[3])
-        turn_e(3, 4)
-        quantise_e(3, 4)
-        weight_gradient(3, 1, None)
+        weight_gradient(1, 1, E_LAST_AT + KIB - LAP)
+        weight_gradient(2, 2, None)
+        weight_gradient(3, 3, None)

@@ -95,8 +95,7 @@ def tile_attend_gtower_sil_EW_kernel(tc, eT, W, xT, G, hT, cf, ts, offs, out_0, 
         g_rows = G.rearrange("(p j) i -> p j i", j=PACK)
         g_raw = sbuf([P, PACK, N], F32, "g_raw")
         w_rows = W.rearrange("(p a c) f -> a p c f", a=2, c=2)
-        w_first = [sbuf([P, N], F32, "w_first%d" % c) for c in range(2)]
-        w_second = sbuf([P, 2, N], F32, "w_second")
+        w_raw = [sbuf([P, 2, N], F32, "w_raw%d" % a) for a in range(2)]
         out_0_rows = out_0.rearrange("(p c) n -> c p n", c=TILES)
         e_win = sbuf([P, ITEMS], F32, "e_win", E_AT[1])
         e_sides = {
@@ -115,12 +114,11 @@ def tile_attend_gtower_sil_EW_kernel(tc, eT, W, xT, G, hT, cf, ts, offs, out_0, 
         nc.sync.dma_start(h_win[1][:], h_rows[1])
         nc.sync.dma_start(h_win[2][:], h_rows[2])
         nc.sync.dma_start(h_win[3][:], h_rows[3])
-        nc.sync.dma_start(w_first[0][:], w_rows[0][:, 0, :])
         nc.sync.dma_start(cf_col[:], cf.rearrange("(p t) o -> p (t o)", t=PACK))
-        nc.sync.dma_start(w_first[1][:], w_rows[0][:, 1, :])
-        nc.sync.dma_start(e_sides[0][0][:], eT[block(0), side(0)])
-        nc.sync.dma_start(w_second[:], w_rows[1])
-        nc.sync.dma_start(e_sides[0][1][:], eT[block(0), side(1)])
+        for a in range(2):
+            nc.sync.dma_start(w_raw[a][:], w_rows[a])
+        for a in range(2):
+            nc.sync.dma_start(e_sides[0][a][:], eT[block(0), side(a)])
         nc.sync.dma_start(e_win[:], eT[block(1), :])
         for c in range(2, TILES):
             for a in range(2):
@@ -138,7 +136,7 @@ def tile_attend_gtower_sil_EW_kernel(tc, eT, W, xT, G, hT, cf, ts, offs, out_0, 
 
         h = {}
         s = {}
-        slope = [sbuf([P, N], F32, "slope%d" % t, H_AT[2] if t == 1 else None) for t in range(PACK)]
+        slope = [sbuf([P, N], F32, "slope%d" % t, H_AT[2] + (t - 1) * 2 * KIB if t in (1, 2) else None) for t in range(PACK)]
 
         def gather_h(t, pieces=(everything,), tag=None, s_tag=None):
             s[t] = sbuf([P, N], F32, "s%d" % t, s_tag)
@@ -199,12 +197,12 @@ def tile_attend_gtower_sil_EW_kernel(tc, eT, W, xT, G, hT, cf, ts, offs, out_0, 
         for c, t in [(c, t) for c in range(2) for t in range(PACK)] + [(c, t) for t in range(PACK) for c in range(2, TILES)]:
             nc.tensor.transpose(dv[t][:, block(c)], dv_ts[c][:, block(t)], ident[:])
 
-        w_woven = [sbuf([P, HALF, PACK], BF16, "w_woven%d" % a, at) for a, at in enumerate((None, E_AT[0] + 4 * KIB))]
+        w_woven = [sbuf([P, HALF, PACK], BF16, "w_woven%d" % a, at) for a, at in enumerate((H_AT[3] + 4 * KIB, H_AT[3] + 6 * KIB))]
 
-        def turn_w(c, rows):
+        def turn_w(c):
             turned = psum([P, PACK, P], "w_turned%d" % c, 4 + c)
             for t in range(PACK):
-                nc.tensor.transpose(turned[:, t, :], rows[:, t:N:PACK], ident[:])
+                nc.tensor.transpose(turned[:, t, :], w_raw[c // 2][:, c % 2, t:N:PACK], ident[:])
             nc.scalar.copy(w_woven[c // 2][:, block(c % 2), :], turned[:].rearrange("s t m -> s m t"))
 
         e_half = {c: sbuf([P, ITEMS], BF16, "e_half%d" % c, E_HALF_AT[c]) for c in range(TILES) if c not in E_ON_VECTOR}
@@ -212,7 +210,7 @@ def tile_attend_gtower_sil_EW_kernel(tc, eT, W, xT, G, hT, cf, ts, offs, out_0, 
         def cast_e(c, a):
             nc.scalar.activation(e_half[c][:, side(a)], e_sides[c][a][:], ACT.Copy)
 
-        dz = sbuf([P, PACK * N], BF16, "dz", "part1")
+        dz = sbuf([P, PACK * N], BF16, "dz", H_AT[3])
 
         def make_dz(t, cols=everything):
             nc.vector.scalar_tensor_tensor(
@@ -221,36 +219,34 @@ def tile_attend_gtower_sil_EW_kernel(tc, eT, W, xT, G, hT, cf, ts, offs, out_0, 
 
         for a in range(2):
             make_part(1, half(a))
-        clear_window("x_woven")
-        gather_h(2, (half(0), half(1)))
+        gather_h(2)
+        s_less_one = sbuf([P, N], F32, "s_less_one")
+        nc.scalar.activation(s_less_one[:], s[2][:], ACT.Copy, bias=-1.0)
+        nc.gpsimd.tensor_tensor(part[2][:], s_less_one[:], h[2][:], ALU.mult)
+        clear_window("s_less_one")
         make_slope(1)
-        for a in range(2):
-            make_part(2, half(a))
+        gather_h(3, (half(0), half(1)), H_AT[2] + 2 * KIB)
         make_dz(0)
-        make_slope(2)
-        for c in range(2):
-            turn_w(c, w_first[c][:])
-        gather_h(3, (half(0), half(1)), H_AT[2] + 2 * KIB, "w_first1")
-        make_dz(1)
         for a in range(2):
             make_part(3, half(a))
+        make_dz(1)
+        make_slope(2)
+        make_slope(3)
         make_dz(2)
-        for step in (make_slope, make_dz):
-            for a in range(2):
-                step(3, half(a))
+        make_dz(3)
 
+        for c in range(TILES):
+            turn_w(c)
         for a in range(2):
             cast_e(0, a)
-        for c in range(2, TILES):
-            turn_w(c, w_second[:, c - 2, :])
 
         dzf_mx = mx_tiles(N, "dzf")
         dz_planes = dz[:].rearrange("p (t i) -> p t i", t=PACK)
         dz_f = [sbuf([P, HALF, PACK], BF16, "dz_f%d" % a) for a in range(2)]
+        w_mx = [mx_tiles(HALF, "w0", H_AT[2] + 2 * KIB)]
+        quantise(w_mx[0], half(0), w_woven[0][:].rearrange("s m t -> s (m t)"), E4M3)
         for a in range(2):
             weave(dz_f[a], dz_planes[:, :, half(a)])
-        w_mx = [mx_tiles(HALF, "w0", "slope3")]
-        quantise(w_mx[0], half(0), w_woven[0][:].rearrange("s m t -> s (m t)"), E4M3)
         for a in range(2):
             quantise(dzf_mx, half(a), dz_f[a][:].rearrange("p i t -> p (i t)"), E5M2)
 
@@ -258,7 +254,7 @@ def tile_attend_gtower_sil_EW_kernel(tc, eT, W, xT, G, hT, cf, ts, offs, out_0, 
         dz_words = dz[:].bitcast(F32).rearrange("p (t w) -> p t w", t=PACK)
         dz_i_words = dz_i[:].bitcast(F32).rearrange("s (p t u) -> s p t u", t=PACK, u=2)
         for b in range(2):
-            turned = psum([P, 2, 2, P], "dz_turned%d" % b, b)
+            turned = psum([P, 2, 2, P], "dz_turned%d" % b, 6 + b)
             for t in range(2):
                 for u in range(2):
                     nc.tensor.transpose(turned[:, t, u, :], dz_words[:, 2 * b + t, u:HALF:2], ident[:])
@@ -305,18 +301,18 @@ def tile_attend_gtower_sil_EW_kernel(tc, eT, W, xT, G, hT, cf, ts, offs, out_0, 
             nc.scalar.copy(dw[:], acc[:])
             nc.scalar.dma_start(out_1[block(c), :], dw[:])
 
-        gather_e(0)
+        gather_e(0, H_AT[3])
         gather_e(1, "dz_f0")
-        table_gradient(0, 2, E_AT[1])
-        table_gradient(1, 3, E_AT[1] + 6 * KIB)
+        table_gradient(0, 6, E_AT[1])
+        table_gradient(1, 7, E_AT[1] + 6 * KIB)
         w_mx.append(mx_tiles(HALF, "w1", E_AT[1] + 2 * KIB))
         quantise(w_mx[1], half(0), w_woven[1][:].rearrange("s m t -> s (m t)"), E4M3)
         dzi_mx = mx_tiles(N, "dzi", E_AT[1] + 4 * KIB)
         quantise(dzi_mx, everything, dz_i[:], E5M2)
         scatter(0)
         scatter(1)
-        turn_e(0, 2)
-        turn_e(1, 3)
+        turn_e(0, 6)
+        turn_e(1, 7)
         for a in range(2):
             cast_e(2, a)
         gather_e(2)
@@ -329,10 +325,10 @@ def tile_attend_gtower_sil_EW_kernel(tc, eT, W, xT, G, hT, cf, ts, offs, out_0, 
             cast_e(3, a)
         gather_e(3, E_LAST_AT)
         weight_gradient(0, 0, E_HALF_AT[3])
-        turn_e(3, 7)
-        table_gradient(3, 6, E_LAST_AT - 2 * KIB + LAP)
+        turn_e(3, 2)
+        table_gradient(3, 1, E_LAST_AT - 2 * KIB + LAP)
         quantise_e(2, 4)
         scatter(3)
-        weight_gradient(1, 1, E_LAST_AT + KIB - LAP)
-        weight_gradient(2, 2, None)
-        weight_gradient(3, 3, None)
+        weight_gradient(1, 3, E_LAST_AT + KIB - LAP)
+        weight_gradient(2, 4, None)
+        weight_gradient(3, 5, None)

@@ -113,8 +113,8 @@ def tile_attend_gtower_sil_EW_kernel(tc, eT, W, xT, G, hT, cf, ts, offs, out_0, 
         nc.sync.dma_start(g_raw[:], g_rows)
         nc.sync.dma_start(h_win[1][:], h_rows[1])
         nc.sync.dma_start(h_win[2][:], h_rows[2])
-        nc.sync.dma_start(h_win[3][:], h_rows[3])
         nc.sync.dma_start(cf_col[:], cf.rearrange("(p t) o -> p (t o)", t=PACK))
+        nc.sync.dma_start(h_win[3][:], h_rows[3])
         for a in range(2):
             nc.sync.dma_start(w_raw[a][:], w_rows[a])
         for a in range(2):
@@ -136,7 +136,7 @@ def tile_attend_gtower_sil_EW_kernel(tc, eT, W, xT, G, hT, cf, ts, offs, out_0, 
 
         h = {}
         s = {}
-        slope = [sbuf([P, N], F32, "slope%d" % t, H_AT[2] + (t - 1) * 2 * KIB if t in (1, 2) else None) for t in range(PACK)]
+        slope = [sbuf([P, N], F32, "slope%d" % t, H_AT[2] if t == 1 else None) for t in range(PACK)]
 
         def gather_h(t, pieces=(everything,), tag=None, s_tag=None):
             s[t] = sbuf([P, N], F32, "s%d" % t, s_tag)
@@ -197,7 +197,7 @@ def tile_attend_gtower_sil_EW_kernel(tc, eT, W, xT, G, hT, cf, ts, offs, out_0, 
         for c, t in [(c, t) for c in range(2) for t in range(PACK)] + [(c, t) for t in range(PACK) for c in range(2, TILES)]:
             nc.tensor.transpose(dv[t][:, block(c)], dv_ts[c][:, block(t)], ident[:])
 
-        w_woven = [sbuf([P, HALF, PACK], BF16, "w_woven%d" % a, at) for a, at in enumerate((H_AT[3] + 4 * KIB, H_AT[3] + 6 * KIB))]
+        w_woven = [sbuf([P, HALF, PACK], BF16, "w_woven%d" % a) for a in range(2)]
 
         def turn_w(c):
             turned = psum([P, PACK, P], "w_turned%d" % c, 4 + c)
@@ -210,7 +210,7 @@ def tile_attend_gtower_sil_EW_kernel(tc, eT, W, xT, G, hT, cf, ts, offs, out_0, 
         def cast_e(c, a):
             nc.scalar.activation(e_half[c][:, side(a)], e_sides[c][a][:], ACT.Copy)
 
-        dz = sbuf([P, PACK * N], BF16, "dz", H_AT[3])
+        dz = sbuf([P, PACK * N], BF16, "dz", H_AT[2] + 4 * KIB)
 
         def make_dz(t, cols=everything):
             nc.vector.scalar_tensor_tensor(
@@ -219,21 +219,26 @@ def tile_attend_gtower_sil_EW_kernel(tc, eT, W, xT, G, hT, cf, ts, offs, out_0, 
 
         for a in range(2):
             make_part(1, half(a))
-        gather_h(2)
-        s_less_one = sbuf([P, N], F32, "s_less_one")
-        nc.scalar.activation(s_less_one[:], s[2][:], ACT.Copy, bias=-1.0)
-        nc.gpsimd.tensor_tensor(part[2][:], s_less_one[:], h[2][:], ALU.mult)
-        clear_window("s_less_one")
+        gather_h(2, (half(0), half(1)))
         make_slope(1)
-        gather_h(3, (half(0), half(1)), H_AT[2] + 2 * KIB)
-        make_dz(0)
+        clear_window("part1")
         for a in range(2):
-            make_part(3, half(a))
-        make_dz(1)
+            make_part(2, half(a))
+        make_dz(0)
         make_slope(2)
-        make_slope(3)
+        make_dz(1)
         make_dz(2)
-        make_dz(3)
+        s[3] = sbuf([P, N], F32, "s3")
+        last_less_one = sbuf([P, N], F32, "last_less_one")
+        for a in range(2):
+            nc.scalar.activation(s[3][:, half(a)], listed(h_win[3], half(a)), ACT.Sigmoid)
+            nc.scalar.activation(last_less_one[:, half(a)], s[3][:, half(a)], ACT.Copy, bias=-1.0)
+        for a in range(2):
+            nc.vector.tensor_tensor(part[3][:, half(a)], listed(h_win[3], half(a)), last_less_one[:, half(a)], ALU.mult)
+        for a in range(2):
+            make_slope(3, half(a))
+        for a in range(2):
+            make_dz(3, half(a))
 
         for c in range(TILES):
             turn_w(c)
@@ -243,7 +248,7 @@ def tile_attend_gtower_sil_EW_kernel(tc, eT, W, xT, G, hT, cf, ts, offs, out_0, 
         dzf_mx = mx_tiles(N, "dzf")
         dz_planes = dz[:].rearrange("p (t i) -> p t i", t=PACK)
         dz_f = [sbuf([P, HALF, PACK], BF16, "dz_f%d" % a) for a in range(2)]
-        w_mx = [mx_tiles(HALF, "w0", H_AT[2] + 2 * KIB)]
+        w_mx = [mx_tiles(HALF, "w0", "part3")]
         quantise(w_mx[0], half(0), w_woven[0][:].rearrange("s m t -> s (m t)"), E4M3)
         for a in range(2):
             weave(dz_f[a], dz_planes[:, :, half(a)])
@@ -301,7 +306,7 @@ def tile_attend_gtower_sil_EW_kernel(tc, eT, W, xT, G, hT, cf, ts, offs, out_0, 
             nc.scalar.copy(dw[:], acc[:])
             nc.scalar.dma_start(out_1[block(c), :], dw[:])
 
-        gather_e(0, H_AT[3])
+        gather_e(0, H_AT[2] + 4 * KIB)
         gather_e(1, "dz_f0")
         table_gradient(0, 6, E_AT[1])
         table_gradient(1, 7, E_AT[1] + 6 * KIB)

@@ -27,6 +27,7 @@ H_AT = [0, 8 * KIB, 16 * KIB, 24 * KIB]
 E_AT = [32 * KIB, 42 * KIB, 50 * KIB, 58 * KIB]
 E_HALF_AT = {0: 74 * KIB, 2: 66 * KIB, 3: 70 * KIB}
 E_LAST_AT = 80 * KIB
+DZ_AT = 84 * KIB
 LAP = 64
 SIDE = ITEMS // 2
 
@@ -67,8 +68,8 @@ def tile_attend_gtower_sil_EW_kernel(tc, eT, W, xT, G, hT, cf, ts, offs, out_0, 
                 stop=True,
             )
 
-        def weave(woven, planes):
-            nc.vector.tensor_copy(
+        def weave(woven, planes, copy=nc.vector.tensor_copy):
+            copy(
                 woven[:].rearrange("p (c i) t -> p c t i", i=PACK), planes.rearrange("p t (c i) -> p c t i", i=PACK)
             )
 
@@ -90,8 +91,7 @@ def tile_attend_gtower_sil_EW_kernel(tc, eT, W, xT, G, hT, cf, ts, offs, out_0, 
 
         h_rows = hT.rearrange("(p t) n -> t p n", t=PACK)
         h_win = [sbuf([P, ITEMS], F32, "h_win%d" % t, H_AT[t]) for t in range(PACK)]
-        x_rows = xT.rearrange("(p a c) r -> a p c r", a=2, c=2)
-        x_raw = [sbuf([P, 2, N], F32, "x_raw%d" % a) for a in range(2)]
+        x_raw = sbuf([P, PACK, N], F32, "x_raw")
         g_rows = G.rearrange("(p j) i -> p j i", j=PACK)
         g_raw = sbuf([P, PACK, N], F32, "g_raw")
         w_rows = W.rearrange("(p a c) f -> a p c f", a=2, c=2)
@@ -104,16 +104,16 @@ def tile_attend_gtower_sil_EW_kernel(tc, eT, W, xT, G, hT, cf, ts, offs, out_0, 
         ts_win = sbuf([P, ITEMS], F32, "ts_win")
         cf_col = sbuf([P, PACK], F32, "cf_col")
 
-        nc.gpsimd.memset(ts_win[:], 0.0)
-        nc.sync.dma_start(h_win[0][:], h_rows[0])
+        nc.gpsimd.memset(ts_win[:, side(0)], 0.0)
+        nc.vector.memset(ts_win[:, side(1)], 0.0)
+        nc.sync.dma_start(x_raw[:], xT.rearrange("(p t) r -> p t r", t=PACK))
         nc.sync.dma_start(offsets[:], offs)
+        nc.sync.dma_start(cf_col[:], cf.rearrange("(p t) o -> p (t o)", t=PACK))
         nc.sync.dma_start(ts_win[0:1, :], ts[0:1, :])
-        for a in range(2):
-            nc.sync.dma_start(x_raw[a][:], x_rows[a])
         nc.sync.dma_start(g_raw[:], g_rows)
+        nc.sync.dma_start(h_win[0][:], h_rows[0])
         nc.sync.dma_start(h_win[1][:], h_rows[1])
         nc.sync.dma_start(h_win[2][:], h_rows[2])
-        nc.sync.dma_start(cf_col[:], cf.rearrange("(p t) o -> p (t o)", t=PACK))
         nc.sync.dma_start(h_win[3][:], h_rows[3])
         for a in range(2):
             nc.sync.dma_start(w_raw[a][:], w_rows[a])
@@ -126,17 +126,18 @@ def tile_attend_gtower_sil_EW_kernel(tc, eT, W, xT, G, hT, cf, ts, offs, out_0, 
 
         ident = sbuf([P, P], F32, "ident")
         make_identity(nc, ident[:])
+        warm_up = sbuf([P, 2], F32, "warm_up")
+        nc.vector.memset(warm_up[:, 0:1], 0.0)
+        nc.scalar.activation(warm_up[:, 1:2], warm_up[:, 0:1], ACT.Sigmoid)
         windows = []
 
         def clear_window(tag=None):
             windows.append(sbuf([P, ITEMS], F32, "window%d" % len(windows), tag))
             nc.gpsimd.memset(windows[-1][:], 0.0)
 
-        clear_window()
-
         h = {}
         s = {}
-        slope = [sbuf([P, N], F32, "slope%d" % t, H_AT[2] if t == 1 else None) for t in range(PACK)]
+        slope = [sbuf([P, N], F32, "slope%d" % t, H_AT[1] if t == 0 else None) for t in range(PACK)]
 
         def gather_h(t, pieces=(everything,), tag=None, s_tag=None):
             s[t] = sbuf([P, N], F32, "s%d" % t, s_tag)
@@ -153,42 +154,45 @@ def tile_attend_gtower_sil_EW_kernel(tc, eT, W, xT, G, hT, cf, ts, offs, out_0, 
         def make_slope(t, cols=everything):
             nc.vector.scalar_tensor_tensor(slope[t][:, cols], part[t][:, cols], 1.0, s[t][:, cols], ALU.subtract, ALU.mult)
 
-        gather_h(0)
-
-        ts_row = sbuf([P, N], F32, "ts_row")
-        nc.vector.tensor_copy(ts_row[:], listed(ts_win))
-        make_part(0)
-        make_slope(0)
+        def fused_part(t):
+            s[t] = sbuf([P, N], F32, "s%d" % t)
+            less_one = sbuf([P, N], F32, "less_one%d" % t)
+            for a in range(2):
+                nc.scalar.activation(s[t][:, half(a)], listed(h_win[t], half(a)), ACT.Sigmoid)
+                nc.scalar.activation(less_one[:, half(a)], s[t][:, half(a)], ACT.Copy, bias=-1.0)
+            for a in range(2):
+                nc.vector.tensor_tensor(part[t][:, half(a)], listed(h_win[t], half(a)), less_one[:, half(a)], ALU.mult)
 
         x_woven = sbuf([P, N * PACK], BF16, "x_woven")
         x_woven_words = x_woven[:].bitcast(F32).rearrange("s (t m u) -> s t m u", t=PACK, u=2)
+        ts_row = sbuf([P, N], F32, "ts_row")
         for t in range(PACK):
-            x_half = sbuf([P, N], BF16, "x_half%d" % t, H_AT[0] + t * KIB if t > 0 else None)
-            nc.scalar.copy(x_half[:], x_raw[t // 2][:, t % 2, :])
+            x_half = sbuf([P, N], BF16, "x_half%d" % t, "g_woven1" if t == PACK - 1 else None)
+            cast = nc.vector.tensor_copy if t < 2 else nc.scalar.copy
+            cast(x_half[:], x_raw[:, t, :])
             x_words = x_half[:].bitcast(F32)
             turned = psum([P, 2, P], "x_turned%d" % t, t)
             for u in range(2):
                 nc.tensor.transpose(turned[:, u, :], x_words[:, u:HALF:2], ident[:])
             nc.scalar.copy(x_woven_words[:, t, :, :], turned[:].rearrange("s u m -> s m u"))
-        ts_turned = psum([P, TILES, P], "ts_turned", 7)
+
+        nc.vector.tensor_copy(ts_row[:], listed(ts_win))
+        ts_turned = psum([P, TILES, P], "ts_turned", PACK - 1)
         for c in range(TILES):
             nc.tensor.transpose(ts_turned[:, c, :], ts_row[:, block(c)], ident[:])
         ts_col = sbuf([P, TILES], F32, "ts_col")
+        x_mx = mx_tiles(N, "x")
+        g_woven = [sbuf([P, HALF, PACK], BF16, "g_woven%d" % a) for a in range(2)]
+        weave(g_woven[0], g_raw[:, :, half(0)])
+        weave(g_woven[1], g_raw[:, :, half(1)], nc.scalar.copy)
         nc.scalar.activation(ts_col[:], ts_turned[:, :, 0], ACT.Copy, scale=-1.0)
-        g_woven = [sbuf([P, HALF, PACK], BF16, "g_woven%d" % a, "h0" if a == 0 else None) for a in range(2)]
-        for a in range(2):
-            weave(g_woven[a], g_raw[:, :, half(a)])
-        g_mx = [mx_tiles(HALF, "g0")]
-        quantise(g_mx[0], half(0), g_woven[0][:].rearrange("p i j -> p (i j)"), E5M2)
-        x_mx = mx_tiles(N, "x", "g_raw")
         quantise(x_mx, everything, x_woven[:], E4M3)
-        gather_h(1, (half(0), half(1)), "x_woven")
-        g_mx.append(mx_tiles(HALF, "g1", H_AT[1] + 2 * KIB))
+        g_mx = [mx_tiles(HALF, "g%d" % a, at) for a, at in enumerate((None, H_AT[0]))]
+        quantise(g_mx[0], half(0), g_woven[0][:].rearrange("p i j -> p (i j)"), E5M2)
+        gather_h(0, (half(0), half(1)), "g_woven0")
         quantise(g_mx[1], half(0), g_woven[1][:].rearrange("p i j -> p (i j)"), E5M2)
 
-        clear_window("g_woven1")
-
-        dv_ts = [sbuf([P, N], F32, "dv_ts%d" % c, H_AT[1] if c == 0 else None) for c in range(TILES)]
+        dv_ts = [sbuf([P, N], F32, "dv_ts%d" % c, H_AT[0] + 4 * KIB if c == 0 else None) for c in range(TILES)]
         dv = [psum([P, N], "dv%d" % t, t) for t in range(PACK)]
         for c in range(TILES):
             dv_t = psum([P, N], "dv_t%d" % c, 4 + c)
@@ -210,7 +214,7 @@ def tile_attend_gtower_sil_EW_kernel(tc, eT, W, xT, G, hT, cf, ts, offs, out_0, 
         def cast_e(c, a):
             nc.scalar.activation(e_half[c][:, side(a)], e_sides[c][a][:], ACT.Copy)
 
-        dz = sbuf([P, PACK * N], BF16, "dz", H_AT[2] + 4 * KIB)
+        dz = sbuf([P, PACK * N], BF16, "dz", DZ_AT)
 
         def make_dz(t, cols=everything):
             nc.vector.scalar_tensor_tensor(
@@ -218,27 +222,24 @@ def tile_attend_gtower_sil_EW_kernel(tc, eT, W, xT, G, hT, cf, ts, offs, out_0, 
             )
 
         for a in range(2):
+            make_part(0, half(a))
+        clear_window("g_woven1")
+        gather_h(1, (half(0), half(1)), DZ_AT)
+        make_slope(0)
+        clear_window("part0")
+        for a in range(2):
             make_part(1, half(a))
-        gather_h(2, (half(0), half(1)))
-        make_slope(1)
+        for a in range(2):
+            make_slope(1, half(a))
         clear_window("part1")
-        for a in range(2):
-            make_part(2, half(a))
         make_dz(0)
-        make_slope(2)
         make_dz(1)
-        make_dz(2)
-        s[3] = sbuf([P, N], F32, "s3")
-        last_less_one = sbuf([P, N], F32, "last_less_one")
-        for a in range(2):
-            nc.scalar.activation(s[3][:, half(a)], listed(h_win[3], half(a)), ACT.Sigmoid)
-            nc.scalar.activation(last_less_one[:, half(a)], s[3][:, half(a)], ACT.Copy, bias=-1.0)
-        for a in range(2):
-            nc.vector.tensor_tensor(part[3][:, half(a)], listed(h_win[3], half(a)), last_less_one[:, half(a)], ALU.mult)
-        for a in range(2):
-            make_slope(3, half(a))
-        for a in range(2):
-            make_dz(3, half(a))
+        for t in range(2, PACK):
+            fused_part(t)
+            for a in range(2):
+                make_slope(t, half(a))
+            for a in range(2):
+                make_dz(t, half(a))
 
         for c in range(TILES):
             turn_w(c)
@@ -306,7 +307,7 @@ def tile_attend_gtower_sil_EW_kernel(tc, eT, W, xT, G, hT, cf, ts, offs, out_0, 
             nc.scalar.copy(dw[:], acc[:])
             nc.scalar.dma_start(out_1[block(c), :], dw[:])
 
-        gather_e(0, H_AT[2] + 4 * KIB)
+        gather_e(0, DZ_AT)
         gather_e(1, "dz_f0")
         table_gradient(0, 6, E_AT[1])
         table_gradient(1, 7, E_AT[1] + 6 * KIB)

from contextlib import ExitStack

import concourse.mybir as mybir
from concourse.masks import make_identity

F32 = mybir.dt.float32
BF16 = mybir.dt.bfloat16
U32 = mybir.dt.uint32
U16 = mybir.dt.uint16
U8 = mybir.dt.uint8
E4M3 = mybir.dt.float8_e4m3fn_x4
E5M2 = mybir.dt.float8_e5m2_x4
ALU = mybir.AluOpType
ACT = mybir.ActivationFunctionType

P = 128
PACK = 4
N = 512
HALF = N // 2
ITEMS = 2048
TILES = N // P
WINDOWS = 3
E_ON_VECTOR = (1,)

KIB = 1024
H_AT = [0, 8 * KIB, 16 * KIB, 24 * KIB]
E_AT = [32 * KIB, 42 * KIB, 50 * KIB, 58 * KIB]
E_HALF_AT = {0: 74 * KIB, 2: 66 * KIB, 3: 70 * KIB}
E_LAST_AT = 80 * KIB
DZ_AT = 84 * KIB
LAP = 64
SIDE = ITEMS // 2

FLOPS = 3 * 2 * N * N * N
BYTES = 4 * (3 * N * ITEMS + 4 * N * N + ITEMS + N) + 2 * P * (N // 16)


def tile_attend_gtower_sil_EW_kernel(tc, eT, W, xT, G, hT, cf, ts, offs, out_0, out_1):
    nc = tc.nc
    with ExitStack() as ctx:
        lists = ctx.enter_context(tc.tile_pool(name="lists", bufs=1))
        sb = ctx.enter_context(tc.tile_pool(name="sb", bufs=1))
        arena = ctx.enter_context(tc.tile_pool(name="arena", bufs=1))
        ps = ctx.enter_context(tc.psum_pool(name="ps", bufs=1))

        def sbuf(shape, dtype, name, tag=None):
            if isinstance(tag, int):
                return arena.tile(shape, dtype, name=name, align_bytes=64, offset=tag)
            return sb.tile(shape, dtype, name=name, tag=tag or name, align_bytes=64)

        def psum(shape, name, bank):
            return ps.tile(shape, F32, name=name, tag="bank%d" % bank)

        def mx_tiles(width, name, tag=None):
            return sbuf([P, width], U32, name + "_codes", tag), sbuf([P, width], U8, name + "_scales")

        def quantise(mx, cols, woven, fmt):
            nc.vector.quantize_mx(out=mx[0][:, cols].bitcast(fmt), scales=mx[1][:, cols], in_=woven)

        def multiply(acc, still, still_cols, still_fmt, moving, moving_fmt):
            nc.tensor.matmul_mx(
                out=acc,
                lhsT=still[0][:, still_cols].bitcast(still_fmt),
                lhsT_scale=still[1][:, still_cols],
                rhs=moving[0][:].bitcast(moving_fmt),
                rhs_scale=moving[1][:],
                start=True,
                stop=True,
            )

        def weave(woven, planes, copy=nc.vector.tensor_copy):
            copy(
                woven[:].rearrange("p (c i) t -> p c t i", i=PACK), planes.rearrange("p t (c i) -> p c t i", i=PACK)
            )

        def block(c):
            return slice(c * P, (c + 1) * P)

        def half(a):
            return slice(a * HALF, (a + 1) * HALF)

        def side(a):
            return slice(a * SIDE, (a + 1) * SIDE)

        everything = slice(0, N)

        offsets = lists.tile([P, N // 16], U16, name="offsets")

        def listed(window, cols=everything):
            return window[:].indirect(offsets[:, cols.start // 16 : cols.stop // 16])

        h_rows = hT.rearrange("(p t) n -> t p n", t=PACK)
        h_win = [sbuf([P, ITEMS], F32, "h_win%d" % t, H_AT[t]) for t in range(PACK)]
        x_raw = sbuf([P, PACK, N], F32, "x_raw")
        g_rows = G.rearrange("(p j) i -> p j i", j=PACK)
        g_raw = sbuf([P, PACK, N], F32, "g_raw")
        w_rows = W.rearrange("(p a c) f -> a p c f", a=2, c=2)
        w_raw = [sbuf([P, 2, N], F32, "w_raw%d" % a) for a in range(2)]
        out_0_rows = out_0.rearrange("(p c) n -> c p n", c=TILES)
        e_win = sbuf([P, ITEMS], F32, "e_win", E_AT[1])
        e_sides = {
            c: [sbuf([P, SIDE], F32, "e_side%d_%d" % (c, a), E_AT[c] + a * 4 * KIB) for a in range(2)] for c in range(TILES) if c not in E_ON_VECTOR
        }
        ts_win = sbuf([P, ITEMS], F32, "ts_win")
        cf_col = sbuf([P, PACK], F32, "cf_col")

        nc.gpsimd.memset(ts_win[:, side(0)], 0.0)
        nc.vector.memset(ts_win[:, side(1)], 0.0)
        nc.sync.dma_start(x_raw[:], xT.rearrange("(p t) r -> p t r", t=PACK))
        nc.sync.dma_start(offsets[:], offs)
        nc.sync.dma_start(cf_col[:], cf.rearrange("(p t) o -> p (t o)", t=PACK))
        nc.sync.dma_start(ts_win[0:1, :], ts[0:1, :])
        nc.sync.dma_start(g_raw[:], g_rows)
        nc.sync.dma_start(h_win[0][:], h_rows[0])
        nc.sync.dma_start(h_win[1][:], h_rows[1])
        nc.sync.dma_start(h_win[2][:], h_rows[2])
        nc.sync.dma_start(h_win[3][:], h_rows[3])
        for a in range(2):
            nc.sync.dma_start(w_raw[a][:], w_rows[a])
        for a in range(2):
            nc.sync.dma_start(e_sides[0][a][:], eT[block(0), side(a)])
        nc.sync.dma_start(e_win[:], eT[block(1), :])
        for c in range(2, TILES):
            for a in range(2):
                nc.sync.dma_start(e_sides[c][a][:], eT[block(c), side(a)])

        ident = sbuf([P, P], F32, "ident")
        make_identity(nc, ident[:])
        warm_up = sbuf([P, 2], F32, "warm_up")
        nc.vector.memset(warm_up[:, 0:1], 0.0)
        nc.scalar.activation(warm_up[:, 1:2], warm_up[:, 0:1], ACT.Sigmoid)
        windows = []

        def clear_window(tag=None):
            windows.append(sbuf([P, ITEMS], F32, "window%d" % len(windows), tag))
            nc.gpsimd.memset(windows[-1][:], 0.0)

        h = {}
        s = {}
        slope = [sbuf([P, N], F32, "slope%d" % t, H_AT[1] if t == 0 else None) for t in range(PACK)]

        def gather_h(t, pieces=(everything,), tag=None, s_tag=None):
            s[t] = sbuf([P, N], F32, "s%d" % t, s_tag)
            h[t] = sbuf([P, N], F32, "h%d" % t, tag)
            for cols in pieces:
                nc.vector.tensor_copy(h[t][:, cols], listed(h_win[t], cols))
                nc.scalar.activation(s[t][:, cols], h[t][:, cols], ACT.Sigmoid)

        part = [sbuf([P, N], F32, "part%d" % t) for t in range(PACK)]

        def make_part(t, cols=everything):
            nc.vector.scalar_tensor_tensor(part[t][:, cols], s[t][:, cols], 1.0, h[t][:, cols], ALU.subtract, ALU.mult)

        def make_slope(t, cols=everything):
            nc.vector.scalar_tensor_tensor(slope[t][:, cols], part[t][:, cols], 1.0, s[t][:, cols], ALU.subtract, ALU.mult)

        def fused_part(t):
            s[t] = sbuf([P, N], F32, "s%d" % t)
            less_one = sbuf([P, N], F32, "less_one%d" % t)
            for a in range(2):
                nc.scalar.activation(s[t][:, half(a)], listed(h_win[t], half(a)), ACT.Sigmoid)
                nc.scalar.activation(less_one[:, half(a)], s[t][:, half(a)], ACT.Copy, bias=-1.0)
            for a in range(2):
                nc.vector.tensor_tensor(part[t][:, half(a)], listed(h_win[t], half(a)), less_one[:, half(a)], ALU.mult)

        x_woven = sbuf([P, N * PACK], BF16, "x_woven")
        x_woven_words = x_woven[:].bitcast(F32).rearrange("s (t m u) -> s t m u", t=PACK, u=2)
        ts_row = sbuf([P, N], F32, "ts_row")
        for t in range(PACK):
            x_half = sbuf([P, N], BF16, "x_half%d" % t, "g_woven1" if t == PACK - 1 else None)
            cast = nc.vector.tensor_copy if t < 2 else nc.scalar.copy
            cast(x_half[:], x_raw[:, t, :])
            x_words = x_half[:].bitcast(F32)
            turned = psum([P, 2, P], "x_turned%d" % t, t)
            for u in range(2):
                nc.tensor.transpose(turned[:, u, :], x_words[:, u:HALF:2], ident[:])
            nc.scalar.copy(x_woven_words[:, t, :, :], turned[:].rearrange("s u m -> s m u"))

        nc.vector.tensor_copy(ts_row[:], listed(ts_win))
        ts_turned = psum([P, TILES, P], "ts_turned", PACK - 1)
        for c in range(TILES):
            nc.tensor.transpose(ts_turned[:, c, :], ts_row[:, block(c)], ident[:])
        ts_col = sbuf([P, TILES], F32, "ts_col")
        x_mx = mx_tiles(N, "x")
        g_woven = [sbuf([P, HALF, PACK], BF16, "g_woven%d" % a) for a in range(2)]
        weave(g_woven[0], g_raw[:, :, half(0)])
        weave(g_woven[1], g_raw[:, :, half(1)], nc.scalar.copy)
        nc.scalar.activation(ts_col[:], ts_turned[:, :, 0], ACT.Copy, scale=-1.0)
        quantise(x_mx, everything, x_woven[:], E4M3)
        g_mx = [mx_tiles(HALF, "g%d" % a, at) for a, at in enumerate((None, H_AT[0]))]
        quantise(g_mx[0], half(0), g_woven[0][:].rearrange("p i j -> p (i j)"), E5M2)
        gather_h(0, (half(0), half(1)), "g_woven0")
        quantise(g_mx[1], half(0), g_woven[1][:].rearrange("p i j -> p (i j)"), E5M2)

        dv_ts = [sbuf([P, N], F32, "dv_ts%d" % c, H_AT[0] + 4 * KIB if c == 0 else None) for c in range(TILES)]
        dv = [psum([P, N], "dv%d" % t, t) for t in range(PACK)]
        for c in range(TILES):
            dv_t = psum([P, N], "dv_t%d" % c, 4 + c)
            multiply(dv_t[:], g_mx[c // 2], block(c % 2), E5M2, x_mx, E4M3)
            nc.scalar.activation(dv_ts[c][:], dv_t[:], ACT.Copy, scale=ts_col[:, c : c + 1])
        for c, t in [(c, t) for c in range(2) for t in range(PACK)] + [(c, t) for t in range(PACK) for c in range(2, TILES)]:
            nc.tensor.transpose(dv[t][:, block(c)], dv_ts[c][:, block(t)], ident[:])

        w_woven = [sbuf([P, HALF, PACK], BF16, "w_woven%d" % a) for a in range(2)]

        def turn_w(c):
            turned = psum([P, PACK, P], "w_turned%d" % c, 4 + c)
            for t in range(PACK):
                nc.tensor.transpose(turned[:, t, :], w_raw[c // 2][:, c % 2, t:N:PACK], ident[:])
            nc.scalar.copy(w_woven[c // 2][:, block(c % 2), :], turned[:].rearrange("s t m -> s m t"))

        e_half = {c: sbuf([P, ITEMS], BF16, "e_half%d" % c, E_HALF_AT[c]) for c in range(TILES) if c not in E_ON_VECTOR}

        def cast_e(c, a):
            nc.scalar.activation(e_half[c][:, side(a)], e_sides[c][a][:], ACT.Copy)

        dz = sbuf([P, PACK * N], BF16, "dz", DZ_AT)

        def make_dz(t, cols=everything):
            nc.vector.scalar_tensor_tensor(
                dz[:, t * N + cols.start : t * N + cols.stop], dv[t][:, cols], cf_col[:, t : t + 1], slope[t][:, cols], ALU.mult, ALU.mult
            )

        for a in range(2):
            make_part(0, half(a))
        clear_window("g_woven1")
        gather_h(1, (half(0), half(1)), DZ_AT)
        make_slope(0)
        clear_window("part0")
        for a in range(2):
            make_part(1, half(a))
        for a in range(2):
            make_slope(1, half(a))
        clear_window("part1")
        make_dz(0)
        make_dz(1)
        for t in range(2, PACK):
            fused_part(t)
            for a in range(2):
                make_slope(t, half(a))
            for a in range(2):
                make_dz(t, half(a))

        for c in range(TILES):
            turn_w(c)
        for a in range(2):
            cast_e(0, a)

        dzf_mx = mx_tiles(N, "dzf")
        dz_planes = dz[:].rearrange("p (t i) -> p t i", t=PACK)
        dz_f = [sbuf([P, HALF, PACK], BF16, "dz_f%d" % a) for a in range(2)]
        w_mx = [mx_tiles(HALF, "w0", "part3")]
        quantise(w_mx[0], half(0), w_woven[0][:].rearrange("s m t -> s (m t)"), E4M3)
        for a in range(2):
            weave(dz_f[a], dz_planes[:, :, half(a)])
        for a in range(2):
            quantise(dzf_mx, half(a), dz_f[a][:].rearrange("p i t -> p (i t)"), E5M2)

        dz_i = sbuf([P, N * PACK], BF16, "dz_i", E_AT[0] + 6 * KIB)
        dz_words = dz[:].bitcast(F32).rearrange("p (t w) -> p t w", t=PACK)
        dz_i_words = dz_i[:].bitcast(F32).rearrange("s (p t u) -> s p t u", t=PACK, u=2)
        for b in range(2):
            turned = psum([P, 2, 2, P], "dz_turned%d" % b, 6 + b)
            for t in range(2):
                for u in range(2):
                    nc.tensor.transpose(turned[:, t, u, :], dz_words[:, 2 * b + t, u:HALF:2], ident[:])
            nc.scalar.copy(dz_i_words[:, :, 2 * b : 2 * b + 2, :], turned[:].rearrange("s t u p -> s p t u"))

        e = {}

        def gather_e(c, tag=None):
            e[c] = sbuf([P, N], BF16, "e%d" % c, tag)
            if c in E_ON_VECTOR:
                nc.vector.tensor_copy(e[c][:], listed(e_win))
            else:
                nc.scalar.activation(e[c][:], listed(e_half[c]), ACT.Copy)

        e_woven = sbuf([P, TILES * HALF], F32, "e_woven")

        def turn_e(c, bank):
            e_words = e[c][:].bitcast(F32)
            turned = psum([P, 2, P], "e_turned%d" % c, bank)
            for u in range(2):
                nc.tensor.transpose(turned[:, u, :], e_words[:, u:HALF:2], ident[:])
            nc.scalar.copy(e_woven[:, half(c)].rearrange("s (d u) -> s d u", u=2), turned[:].rearrange("s u m -> s m u"))

        de = {}

        def table_gradient(c, bank, tag=None):
            de_acc = psum([P, N], "de_acc%d" % c, bank)
            multiply(de_acc[:], w_mx[c // 2], block(c % 2), E4M3, dzf_mx, E5M2)
            de[c] = sbuf([P, N], F32, "de%d" % c, tag)
            nc.scalar.copy(de[c][:], de_acc[:])

        def scatter(c):
            window = windows[c % WINDOWS]
            nc.vector.tensor_copy(listed(window), de[c][:])
            nc.sync.dma_start(out_0_rows[c], window[:])

        def quantise_e(first, end):
            quantise(e_mx, slice(first * P, end * P), e_woven[:, first * HALF : end * HALF].bitcast(BF16), E4M3)

        def weight_gradient(c, bank, tag):
            acc = psum([P, N], "dw_acc%d" % c, bank)
            multiply(acc[:], e_mx, block(c), E4M3, dzi_mx, E5M2)
            dw = sbuf([P, N], F32, "dw%d" % c, tag)
            nc.scalar.copy(dw[:], acc[:])
            nc.scalar.dma_start(out_1[block(c), :], dw[:])

        gather_e(0, DZ_AT)
        gather_e(1, "dz_f0")
        table_gradient(0, 6, E_AT[1])
        table_gradient(1, 7, E_AT[1] + 6 * KIB)
        w_mx.append(mx_tiles(HALF, "w1", E_AT[1] + 2 * KIB))
        quantise(w_mx[1], half(0), w_woven[1][:].rearrange("s m t -> s (m t)"), E4M3)
        dzi_mx = mx_tiles(N, "dzi", E_AT[1] + 4 * KIB)
        quantise(dzi_mx, everything, dz_i[:], E5M2)
        scatter(0)
        scatter(1)
        turn_e(0, 6)
        turn_e(1, 7)
        for a in range(2):
            cast_e(2, a)
        gather_e(2)
        e_mx = mx_tiles(N, "e", E_HALF_AT[2])
        quantise_e(0, 2)
        table_gradient(2, 5, E_HALF_AT[2] + 2 * KIB)
        scatter(2)
        turn_e(2, 4)
        for a in range(2):
            cast_e(3, a)
        gather_e(3, E_LAST_AT)
        weight_gradient(0, 0, E_HALF_AT[3])
        turn_e(3, 2)
        table_gradient(3, 1, E_LAST_AT - 2 * KIB + LAP)
        quantise_e(2, 4)
        scatter(3)
        weight_gradient(1, 3, E_LAST_AT + KIB - LAP)
        weight_gradient(2, 4, None)
        weight_gradient(3, 5, None)
